import numpy as np
import ml_dtypes


def mxq(x, axis, fmt="e4m3"):
    dtype, down = {"e4m3": (ml_dtypes.float8_e4m3fn, 7), "e5m2": (ml_dtypes.float8_e5m2, 14)}[fmt]
    v = np.moveaxis(np.asarray(x, np.float32).astype(ml_dtypes.bfloat16).astype(np.float64), axis, -1)
    blocks = v.reshape(v.shape[:-1] + (-1, 32))
    amax = np.abs(blocks).max(-1, keepdims=True)
    byte = np.maximum(np.where(amax > 0, np.frexp(amax)[1] - 1 + 127, 0) - down, 1)
    scale = np.exp2(byte - 127.0)
    codes = (blocks / scale).astype(np.float32).astype(dtype).astype(np.float64)
    return np.moveaxis((codes * scale).reshape(v.shape), -1, axis)


WIDE = False


def mx_kscale(k):
    if not WIDE:
        return np.ones(k)
    levels = np.array([10, -10, 5, -5, 0])
    if k % 512:
        return np.exp2(np.random.permutation(np.resize(levels, k // 32))).repeat(32)
    a = np.empty((k // 512, 16))
    for p in range(k // 512):
        a[p, :8] = np.random.permutation(np.resize(levels, 8))
        for g in range(8):
            far = levels[np.abs(levels - a[p, g]) >= 10]
            a[p, g + 8] = far[np.random.randint(len(far))]
    return np.exp2(a.ravel()).repeat(32)


def f64(x):
    return np.asarray(x).astype(np.float64)


def striped(idx):
    return np.tile(idx.reshape(-1, 16).T, (8, 1)).astype(np.uint16)


def unstriped(offs):
    return offs[:16].T.reshape(-1).astype(np.int64)


def pack_weight(w):
    k, n = w.shape
    w = f64(np.asarray(w, np.float32).astype(ml_dtypes.bfloat16)).reshape(k // 32, 32, n)
    amax = np.abs(w).max(1)
    byte = np.clip(np.where(amax > 0, np.frexp(amax)[1] - 1 + 127 - 7, 1), 1, 254)
    scaled = (w * np.exp2(127.0 - byte)[:, None, :]).reshape(k, n).astype(np.float32)
    words = np.ascontiguousarray(scaled.reshape(k // 512, 128, 4, n).transpose(0, 1, 3, 2)).astype(ml_dtypes.float8_e4m3fn).view(np.uint8)
    return words, np.ascontiguousarray(byte.astype(np.uint8).reshape(k // 512, 16, n))


def unpack_weight(words, scales):
    g, p, n, _ = words.shape
    vals = np.ascontiguousarray(words).view(ml_dtypes.float8_e4m3fn).astype(np.float64) * np.repeat(np.exp2(scales.astype(np.float64) - 127.0), 8, axis=1)[..., None]
    return vals.transpose(0, 1, 3, 2).reshape(g * 512, n)


def sigmoid(v):
    return 1.0 / (1.0 + np.exp(-np.maximum(v, -700.0)))


K, T, S, J = 512, 1024, 512, 256


def setup_inputs():
    n = np.random.standard_normal
    s = mx_kscale(K)[:, None]
    part = np.random.uniform(0.2, 0.8, (J, 1))
    packed_xT = pack_weight(n((K, T)) * s)
    return {
        "x_words": packed_xT[0],
        "x_scales": packed_xT[1],
        "hT": (n((K, J)) / np.sqrt(K) / s).astype(np.float32),
        "gT": (n((K, J)) / np.sqrt(K) / s).astype(np.float32),
        "mix": (np.concatenate([part, 1.0 - part], axis=1)).astype(np.float32),
        "offs": striped(np.random.permutation(T)[:S]),
    }


def reference(x_words, x_scales, hT, gT, mix, offs):
    hTq = mxq(f64(hT), 0, "e4m3")
    xq = unpack_weight(x_words, x_scales)[:, unstriped(offs)]
    y = hTq.T @ xq
    p = sigmoid(y)
    gTq = mxq(f64(gT), 0, "e4m3")
    z = gTq.T @ xq
    q = sigmoid(z)
    return f64(mix)[:, 0:1] * p + f64(mix)[:, 1:2] * q

@@ -1,0 +1,151 @@
+from contextlib import ExitStack
+
+import concourse.mybir as mybir
+
+K, T, S, J = 512, 1024, 512, 256
+FLOPS = 2 * 2 * K * J * S
+
+F32 = mybir.dt.float32
+BF16 = mybir.dt.bfloat16
+I32 = mybir.dt.int32
+U32 = mybir.dt.uint32
+U16 = mybir.dt.uint16
+U8 = mybir.dt.uint8
+FP8X4 = mybir.dt.float8_e4m3fn_x4
+MULT = mybir.AluOpType.mult
+ADD = mybir.AluOpType.add
+SIGMOID = mybir.ActivationFunctionType.Sigmoid
+
+P = 128
+PACK = 4
+HALF = S // 2
+
+
+def tile_picked_zmos_sig_p_kernel(tc, x_words, x_scales, hT, gT, mix, offs, out):
+    nc = tc.nc
+    with ExitStack() as ctx:
+        sb = ctx.enter_context(tc.tile_pool(name="sb", bufs=1))
+        ps = ctx.enter_context(tc.psum_pool(name="ps", bufs=1))
+
+        offsets = sb.tile([P, S // 16], U16, name="offsets")
+        table_scales = sb.tile([P, T], U8, name="table_scales", align_bytes=64)
+        table_words = sb.tile([P, T], I32, name="table_words", align_bytes=64)
+        weights = sb.tile([P, 2, 2], F32, name="weights")
+        warm_in = sb.tile([P, 1], F32, name="warm_in")
+        warm_out = sb.tile([P, 1], F32, name="warm_out")
+
+        nc.vector.memset(table_scales[:].bitcast(I32), 0)
+        nc.gpsimd.memset(warm_in[:], 0.0)
+        nc.scalar.activation(warm_out[:], warm_in[:], SIGMOID)
+
+        heads = (hT, gT)
+        raw = {}
+
+        def load(head, a):
+            raw[head, a] = sb.tile([P, PACK, P], F32, name="raw_%d_%d" % (head, a))
+            src = heads[head].rearrange("(p j) c -> p j c", j=PACK)
+            nc.sync.dma_start(out=raw[head, a][:], in_=src[:, :, a * P : (a + 1) * P])
+
+        nc.sync.dma_start(offsets[:], offs)
+        load(0, 0)
+        for q in range(4):
+            nc.sync.dma_start(
+                out=table_scales[32 * q : 32 * q + 4, :].bitcast(I32),
+                in_=x_scales[0, 4 * q : 4 * q + 4, :].bitcast(I32),
+            )
+        nc.sync.dma_start(out=table_words[:], in_=x_words[0].rearrange("p n t -> p (n t)").bitcast(I32))
+        load(1, 0)
+        load(0, 1)
+        load(1, 1)
+        nc.gpsimd.dma_start(out=weights[:], in_=mix.rearrange("(a p) c -> p a c", p=P))
+
+        grouped = {}
+        codes = {}
+        planes = {}
+
+        def cast(head, a, on_scalar):
+            grouped[head, a] = sb.tile([P, P, PACK], BF16, name="grouped_%d_%d" % (head, a), align_bytes=64)
+            dst = grouped[head, a][:].rearrange("p (c i) t -> p c t i", i=4)
+            src = raw[head, a][:].rearrange("p t (c i) -> p c t i", i=4)
+            if on_scalar:
+                nc.scalar.copy(dst, src)
+            else:
+                nc.vector.tensor_copy(dst, src)
+
+        def quantize(head, a):
+            codes[head, a] = sb.tile([P, P], U32, name="codes_%d_%d" % (head, a), align_bytes=64)
+            planes[head, a] = sb.tile([P, P], U8, name="planes_%d_%d" % (head, a), align_bytes=64)
+            nc.vector.quantize_mx(
+                out=codes[head, a][:].bitcast(FP8X4),
+                scales=planes[head, a][:],
+                in_=grouped[head, a][:].rearrange("p c t -> p (c t)"),
+            )
+
+        picked_words = {}
+        picked_scales = {}
+
+        def gather_scales(b):
+            picked_scales[b] = sb.tile([P, HALF], U8, name="picked_scales_%d" % b, align_bytes=64)
+            nc.vector.tensor_copy(picked_scales[b][:], table_scales[:].indirect(offsets[:, 16 * b : 16 * (b + 1)]))
+
+        def gather_words(b):
+            picked_words[b] = sb.tile([P, HALF], U32, name="picked_words_%d" % b, align_bytes=64)
+            nc.vector.tensor_copy(
+                picked_words[b][:], table_words[:].bitcast(U32).indirect(offsets[:, 16 * b : 16 * (b + 1)])
+            )
+
+        prob = {}
+
+        def product(head, a, b):
+            acc = ps.tile([P, HALF], F32, name="acc_%d_%d_%d" % (head, a, b))
+            nc.tensor.matmul_mx(
+                out=acc[:],
+                lhsT=codes[head, a][:].bitcast(FP8X4),
+                lhsT_scale=planes[head, a][:],
+                rhs=picked_words[b][:].bitcast(FP8X4),
+                rhs_scale=picked_scales[b][:],
+                start=True,
+                stop=True,
+            )
+            prob[head, a, b] = sb.tile([P, HALF], F32, name="prob_%d_%d_%d" % (head, a, b))
+            nc.scalar.activation(prob[head, a, b][:], acc[:], SIGMOID)
+
+        part = {}
+
+        def weigh(a, b):
+            part[a, b] = sb.tile([P, HALF], F32, name="part_%d_%d" % (a, b))
+            nc.vector.tensor_scalar(part[a, b][:], prob[0, a, b][:], weights[:, a, 0:1], None, MULT)
+
+        def combine(a, b):
+            res = sb.tile([P, HALF], F32, name="res_%d_%d" % (a, b))
+            nc.vector.scalar_tensor_tensor(res[:], prob[1, a, b][:], weights[:, a, 1:2], part[a, b][:], MULT, ADD)
+            nc.sync.dma_start(out=out[a * P : (a + 1) * P, b * HALF : (b + 1) * HALF], in_=res[:])
+
+        cast(0, 0, True)
+        gather_scales(0)
+        gather_scales(1)
+        quantize(0, 0)
+        gather_words(0)
+        cast(1, 0, True)
+        product(0, 0, 0)
+        gather_words(1)
+        quantize(1, 0)
+        cast(0, 1, False)
+        product(0, 0, 1)
+        product(1, 0, 0)
+        product(1, 0, 1)
+        quantize(0, 1)
+        cast(1, 1, False)
+        weigh(0, 0)
+        quantize(1, 1)
+        product(0, 1, 0)
+        product(0, 1, 1)
+        product(1, 1, 0)
+        product(1, 1, 1)
+        weigh(0, 1)
+        combine(0, 0)
+        combine(0, 1)
+        weigh(1, 0)
+        weigh(1, 1)
+        combine(1, 0)
+        combine(1, 1)

@@ -46,18 +46,18 @@ def tile_picked_zmos_sig_p_kernel(tc, x_words, x_scales, hT, gT, mix, offs, out)
             src = heads[head].rearrange("(p j) c -> p j c", j=PACK)
             nc.sync.dma_start(out=raw[head, a][:], in_=src[:, :, a * P : (a + 1) * P])
 
-        nc.sync.dma_start(offsets[:], offs)
         load(0, 0)
+        nc.sync.dma_start(offsets[:], offs)
         for q in range(4):
             nc.sync.dma_start(
                 out=table_scales[32 * q : 32 * q + 4, :].bitcast(I32),
                 in_=x_scales[0, 4 * q : 4 * q + 4, :].bitcast(I32),
             )
+        load(0, 1)
         nc.sync.dma_start(out=table_words[:], in_=x_words[0].rearrange("p n t -> p (n t)").bitcast(I32))
         load(1, 0)
-        load(0, 1)
         load(1, 1)
-        nc.gpsimd.dma_start(out=weights[:], in_=mix.rearrange("(a p) c -> p a c", p=P))
+        nc.sync.dma_start(out=weights[:], in_=mix.rearrange("(a p) c -> p a c", p=P))
 
         grouped = {}
         codes = {}
@@ -73,7 +73,8 @@ def tile_picked_zmos_sig_p_kernel(tc, x_words, x_scales, hT, gT, mix, offs, out)
                 nc.vector.tensor_copy(dst, src)
 
         def quantize(head, a):
-            codes[head, a] = sb.tile([P, P], U32, name="codes_%d_%d" % (head, a), align_bytes=64)
+            tag = "table_scales" if (head, a) == (0, 0) else "codes_%d_%d" % (head, a)
+            codes[head, a] = sb.tile([P, P], U32, name="codes_%d_%d" % (head, a), tag=tag, align_bytes=64)
             planes[head, a] = sb.tile([P, P], U8, name="planes_%d_%d" % (head, a), align_bytes=64)
             nc.vector.quantize_mx(
                 out=codes[head, a][:].bitcast(FP8X4),
@@ -84,68 +85,76 @@ def tile_picked_zmos_sig_p_kernel(tc, x_words, x_scales, hT, gT, mix, offs, out)
         picked_words = {}
         picked_scales = {}
 
-        def gather_scales(b):
-            picked_scales[b] = sb.tile([P, HALF], U8, name="picked_scales_%d" % b, align_bytes=64)
+        def gather_scales(b, tag):
+            picked_scales[b] = sb.tile([P, HALF], U8, name="picked_scales_%d" % b, tag=tag, align_bytes=64)
             nc.vector.tensor_copy(picked_scales[b][:], table_scales[:].indirect(offsets[:, 16 * b : 16 * (b + 1)]))
 
-        def gather_words(b):
-            picked_words[b] = sb.tile([P, HALF], U32, name="picked_words_%d" % b, align_bytes=64)
+        def gather_words(b, tag):
+            picked_words[b] = sb.tile([P, HALF], U32, name="picked_words_%d" % b, tag=tag, align_bytes=64)
             nc.vector.tensor_copy(
                 picked_words[b][:], table_words[:].bitcast(U32).indirect(offsets[:, 16 * b : 16 * (b + 1)])
             )
 
         prob = {}
 
-        def product(head, a, b):
-            acc = ps.tile([P, HALF], F32, name="acc_%d_%d_%d" % (head, a, b))
-            nc.tensor.matmul_mx(
-                out=acc[:],
-                lhsT=codes[head, a][:].bitcast(FP8X4),
-                lhsT_scale=planes[head, a][:],
-                rhs=picked_words[b][:].bitcast(FP8X4),
-                rhs_scale=picked_scales[b][:],
-                start=True,
-                stop=True,
-            )
-            prob[head, a, b] = sb.tile([P, HALF], F32, name="prob_%d_%d_%d" % (head, a, b))
-            nc.scalar.activation(prob[head, a, b][:], acc[:], SIGMOID)
+        def product(head, a, halves):
+            if halves[0] == 0:
+                if head == 0 and a == 0:
+                    first = sb.tile([P, 2 * S], F32, name="first", tag="raw_1_0")
+                    prob[0, 0] = first[:, 0:S]
+                    prob[0, 1] = first[:, S : 2 * S]
+                if head == 1:
+                    second = sb.tile([P, S], F32, name="second_%d" % a)
+                    prob[1, a] = second[:]
+            acc = ps.tile([P, HALF * len(halves)], F32, name="acc_%d_%d_%d" % (head, a, halves[0]))
+            for i, b in enumerate(halves):
+                nc.tensor.matmul_mx(
+                    out=acc[:, i * HALF : (i + 1) * HALF],
+                    lhsT=codes[head, a][:].bitcast(FP8X4),
+                    lhsT_scale=planes[head, a][:],
+                    rhs=picked_words[b][:].bitcast(FP8X4),
+                    rhs_scale=picked_scales[b][:],
+                    start=True,
+                    stop=True,
+                )
+            cols = slice(halves[0] * HALF, (halves[-1] + 1) * HALF)
+            nc.scalar.activation(prob[head, a][:, cols], acc[:], SIGMOID)
 
         part = {}
 
-        def weigh(a, b):
-            part[a, b] = sb.tile([P, HALF], F32, name="part_%d_%d" % (a, b))
-            nc.vector.tensor_scalar(part[a, b][:], prob[0, a, b][:], weights[:, a, 0:1], None, MULT)
+        def weigh(a):
+            part[a] = sb.tile([P, S], F32, name="part_%d" % a)
+            nc.vector.tensor_scalar(part[a][:], prob[0, a], weights[:, a, 0:1], None, MULT)
 
-        def combine(a, b):
-            res = sb.tile([P, HALF], F32, name="res_%d_%d" % (a, b))
-            nc.vector.scalar_tensor_tensor(res[:], prob[1, a, b][:], weights[:, a, 1:2], part[a, b][:], MULT, ADD)
-            nc.sync.dma_start(out=out[a * P : (a + 1) * P, b * HALF : (b + 1) * HALF], in_=res[:])
+        def combine(a, halves):
+            cols = slice(halves[0] * HALF, (halves[-1] + 1) * HALF)
+            res = sb.tile([P, HALF * len(halves)], F32, name="res_%d_%d" % (a, halves[0]))
+            nc.vector.scalar_tensor_tensor(res[:], prob[1, a][:, cols], weights[:, a, 1:2], part[a][:, cols], MULT, ADD)
+            nc.sync.dma_start(out=out[a * P : (a + 1) * P, cols], in_=res[:])
 
         cast(0, 0, True)
-        gather_scales(0)
-        gather_scales(1)
+        gather_scales(0, "picked_scales_0")
+        gather_scales(1, "picked_scales_1")
+        cast(0, 1, True)
         quantize(0, 0)
-        gather_words(0)
-        cast(1, 0, True)
-        product(0, 0, 0)
-        gather_words(1)
-        quantize(1, 0)
-        cast(0, 1, False)
-        product(0, 0, 1)
-        product(1, 0, 0)
-        product(1, 0, 1)
         quantize(0, 1)
+        gather_words(0, "picked_words_0")
+        gather_words(1, "picked_words_1")
+        cast(1, 0, True)
         cast(1, 1, False)
-        weigh(0, 0)
+        quantize(1, 0)
         quantize(1, 1)
-        product(0, 1, 0)
-        product(0, 1, 1)
-        product(1, 1, 0)
-        product(1, 1, 1)
-        weigh(0, 1)
-        combine(0, 0)
-        combine(0, 1)
-        weigh(1, 0)
-        weigh(1, 1)
-        combine(1, 0)
-        combine(1, 1)
+        product(0, 0, [0])
+        product(0, 1, [0])
+        product(0, 0, [1])
+        product(0, 1, [1])
+        product(1, 0, [0])
+        product(1, 0, [1])
+        product(1, 1, [0])
+        product(1, 1, [1])
+        weigh(0)
+        weigh(1)
+        combine(0, [0])
+        combine(0, [1])
+        combine(1, [0])
+        combine(1, [1])

@@ -30,51 +30,52 @@ def tile_picked_zmos_sig_p_kernel(tc, x_words, x_scales, hT, gT, mix, offs, out)
         offsets = sb.tile([P, S // 16], U16, name="offsets")
         table_scales = sb.tile([P, T], U8, name="table_scales", align_bytes=64)
         table_words = sb.tile([P, T], I32, name="table_words", align_bytes=64)
-        weights = sb.tile([P, 2, 2], F32, name="weights")
+        weights = sb.tile([P, 2, 2], F32, name="weights", align_bytes=64)
         warm_in = sb.tile([P, 1], F32, name="warm_in")
         warm_out = sb.tile([P, 1], F32, name="warm_out")
-
-        nc.vector.memset(table_scales[:].bitcast(I32), 0)
-        nc.gpsimd.memset(warm_in[:], 0.0)
-        nc.scalar.activation(warm_out[:], warm_in[:], SIGMOID)
+        picked_words = sb.tile([P, S], U32, name="picked_words", align_bytes=64)
+        picked_scales = sb.tile([P, S], U8, name="picked_scales", align_bytes=64)
 
         heads = (hT, gT)
         raw = {}
-
-        def load(head, a):
-            raw[head, a] = sb.tile([P, PACK, P], F32, name="raw_%d_%d" % (head, a))
-            src = heads[head].rearrange("(p j) c -> p j c", j=PACK)
-            nc.sync.dma_start(out=raw[head, a][:], in_=src[:, :, a * P : (a + 1) * P])
-
-        load(0, 0)
-        nc.sync.dma_start(offsets[:], offs)
-        for q in range(4):
-            nc.sync.dma_start(
-                out=table_scales[32 * q : 32 * q + 4, :].bitcast(I32),
-                in_=x_scales[0, 4 * q : 4 * q + 4, :].bitcast(I32),
-            )
-        load(0, 1)
-        nc.sync.dma_start(out=table_words[:], in_=x_words[0].rearrange("p n t -> p (n t)").bitcast(I32))
-        load(1, 0)
-        load(1, 1)
-        nc.sync.dma_start(out=weights[:], in_=mix.rearrange("(a p) c -> p a c", p=P))
-
         grouped = {}
         codes = {}
         planes = {}
+        prob = {}
+        part = {}
 
-        def cast(head, a, on_scalar):
-            grouped[head, a] = sb.tile([P, P, PACK], BF16, name="grouped_%d_%d" % (head, a), align_bytes=64)
+        def load(queue, head, a):
+            raw[head, a] = sb.tile([P, PACK, P], F32, name="raw_%d_%d" % (head, a), align_bytes=64)
+            src = heads[head].rearrange("(p j) c -> p j c", j=PACK)
+            queue.dma_start(out=raw[head, a][:], in_=src[:, :, a * P : (a + 1) * P])
+
+        def load_scales(queue, q):
+            queue.dma_start(
+                out=table_scales[32 * q : 32 * q + 4, :].bitcast(I32),
+                in_=x_scales[0, 4 * q : 4 * q + 4, :].bitcast(I32),
+            )
+
+        def load_words(queue):
+            queue.dma_start(out=table_words[:], in_=x_words[0].rearrange("p n t -> p (n t)").bitcast(I32))
+
+        def load_mix(queue):
+            queue.dma_start(out=weights[:], in_=mix.rearrange("(a p) c -> p a c", p=P))
+
+        def cast(head, a, engine, tag=None):
+            name = "grouped_%d_%d" % (head, a)
+            grouped[head, a] = sb.tile([P, P, PACK], BF16, name=name, tag=tag or name, align_bytes=64)
             dst = grouped[head, a][:].rearrange("p (c i) t -> p c t i", i=4)
             src = raw[head, a][:].rearrange("p t (c i) -> p c t i", i=4)
-            if on_scalar:
+            if engine == "scalar":
                 nc.scalar.copy(dst, src)
+            elif engine == "gpsimd":
+                nc.gpsimd.tensor_copy(dst, src)
             else:
                 nc.vector.tensor_copy(dst, src)
 
-        def quantize(head, a):
-            tag = "table_scales" if (head, a) == (0, 0) else "codes_%d_%d" % (head, a)
-            codes[head, a] = sb.tile([P, P], U32, name="codes_%d_%d" % (head, a), tag=tag, align_bytes=64)
+        def quantize(head, a, tag=None):
+            name = "codes_%d_%d" % (head, a)
+            codes[head, a] = sb.tile([P, P], U32, name=name, tag=tag or name, align_bytes=64)
             planes[head, a] = sb.tile([P, P], U8, name="planes_%d_%d" % (head, a), align_bytes=64)
             nc.vector.quantize_mx(
                 out=codes[head, a][:].bitcast(FP8X4),
@@ -82,79 +83,90 @@ def tile_picked_zmos_sig_p_kernel(tc, x_words, x_scales, hT, gT, mix, offs, out)
                 in_=grouped[head, a][:].rearrange("p c t -> p (c t)"),
             )
 
-        picked_words = {}
-        picked_scales = {}
+        def gather_scales(lo, hi):
+            nc.vector.tensor_copy(picked_scales[:, lo:hi], table_scales[:].indirect(offsets[:, lo // 16 : hi // 16]))
 
-        def gather_scales(b, tag):
-            picked_scales[b] = sb.tile([P, HALF], U8, name="picked_scales_%d" % b, tag=tag, align_bytes=64)
-            nc.vector.tensor_copy(picked_scales[b][:], table_scales[:].indirect(offsets[:, 16 * b : 16 * (b + 1)]))
-
-        def gather_words(b, tag):
-            picked_words[b] = sb.tile([P, HALF], U32, name="picked_words_%d" % b, tag=tag, align_bytes=64)
+        def gather_words(lo, hi):
             nc.vector.tensor_copy(
-                picked_words[b][:], table_words[:].bitcast(U32).indirect(offsets[:, 16 * b : 16 * (b + 1)])
+                picked_words[:, lo:hi], table_words[:].bitcast(U32).indirect(offsets[:, lo // 16 : hi // 16])
             )
 
-        prob = {}
+        def warm_up():
+            nc.gpsimd.memset(warm_in[:], 0.0)
+            nc.scalar.activation(warm_out[:], warm_in[:], SIGMOID)
 
-        def product(head, a, halves):
-            if halves[0] == 0:
-                if head == 0 and a == 0:
-                    first = sb.tile([P, 2 * S], F32, name="first", tag="raw_1_0")
-                    prob[0, 0] = first[:, 0:S]
-                    prob[0, 1] = first[:, S : 2 * S]
-                if head == 1:
-                    second = sb.tile([P, S], F32, name="second_%d" % a)
-                    prob[1, a] = second[:]
-            acc = ps.tile([P, HALF * len(halves)], F32, name="acc_%d_%d_%d" % (head, a, halves[0]))
-            for i, b in enumerate(halves):
+        def product(head, a, cuts, tag=None):
+            if not prob:
+                every = sb.tile([P, 4, S], F32, name="prob", tag=tag or "prob", align_bytes=64)
+                for i in range(4):
+                    prob[i % 2, i // 2] = every[:, i, :]
+            lo, hi = cuts[0], cuts[-1]
+            acc = ps.tile([P, hi - lo], F32, name="acc_%d_%d_%d" % (head, a, lo))
+            for c0, c1 in zip(cuts[:-1], cuts[1:]):
                 nc.tensor.matmul_mx(
-                    out=acc[:, i * HALF : (i + 1) * HALF],
+                    out=acc[:, c0 - lo : c1 - lo],
                     lhsT=codes[head, a][:].bitcast(FP8X4),
                     lhsT_scale=planes[head, a][:],
-                    rhs=picked_words[b][:].bitcast(FP8X4),
-                    rhs_scale=picked_scales[b][:],
+                    rhs=picked_words[:, c0:c1].bitcast(FP8X4),
+                    rhs_scale=picked_scales[:, c0:c1],
                     start=True,
                     stop=True,
                 )
-            cols = slice(halves[0] * HALF, (halves[-1] + 1) * HALF)
-            nc.scalar.activation(prob[head, a][:, cols], acc[:], SIGMOID)
+            nc.scalar.activation(prob[head, a][:, lo:hi], acc[:], SIGMOID)
 
-        part = {}
+        def weigh(a, lo, hi, engine=None, tag=None):
+            if a not in part:
+                both = sb.tile([P, 2, S], F32, name="part", tag=tag or "part", align_bytes=64)
+                part[0] = both[:, 0, :]
+                part[1] = both[:, 1, :]
+            (engine or nc.vector).tensor_scalar(
+                part[a][:, lo:hi], prob[0, a][:, lo:hi], weights[:, a, 0:1], None, MULT
+            )
 
-        def weigh(a):
-            part[a] = sb.tile([P, S], F32, name="part_%d" % a)
-            nc.vector.tensor_scalar(part[a][:], prob[0, a], weights[:, a, 0:1], None, MULT)
+        def combine(a, lo, hi, queue=None):
+            res = sb.tile([P, hi - lo], F32, name="res_%d_%d" % (a, lo))
+            nc.vector.scalar_tensor_tensor(
+                res[:], prob[1, a][:, lo:hi], weights[:, a, 1:2], part[a][:, lo:hi], MULT, ADD
+            )
+            (queue or nc.sync).dma_start(out=out[a * P : (a + 1) * P, lo:hi], in_=res[:])
 
-        def combine(a, halves):
-            cols = slice(halves[0] * HALF, (halves[-1] + 1) * HALF)
-            res = sb.tile([P, HALF * len(halves)], F32, name="res_%d_%d" % (a, halves[0]))
-            nc.vector.scalar_tensor_tensor(res[:], prob[1, a][:, cols], weights[:, a, 1:2], part[a][:, cols], MULT, ADD)
-            nc.sync.dma_start(out=out[a * P : (a + 1) * P, cols], in_=res[:])
-
-        cast(0, 0, True)
-        gather_scales(0, "picked_scales_0")
-        gather_scales(1, "picked_scales_1")
-        cast(0, 1, True)
-        quantize(0, 0)
+        nc.vector.memset(table_scales[:].bitcast(I32), 0)
+        warm_up()
+        load(nc.sync, 0, 0)
+        nc.sync.dma_start(offsets[:], offs)
+        load_scales(nc.sync, 0)
+        load_scales(nc.sync, 1)
+        load_scales(nc.sync, 2)
+        load_scales(nc.sync, 3)
+        load(nc.sync, 0, 1)
+        load_words(nc.sync)
+        load(nc.sync, 1, 0)
+        load(nc.sync, 1, 1)
+        load_mix(nc.sync)
+        cast(0, 0, "scalar")
+        gather_scales(0, S)
+        cast(0, 1, "scalar")
+        quantize(0, 0, "raw_0_1")
         quantize(0, 1)
-        gather_words(0, "picked_words_0")
-        gather_words(1, "picked_words_1")
-        cast(1, 0, True)
-        cast(1, 1, False)
+        gather_words(0, HALF)
+        gather_words(HALF, S)
+        cast(1, 0, "scalar")
+        cast(1, 1, "vector")
         quantize(1, 0)
         quantize(1, 1)
-        product(0, 0, [0])
-        product(0, 1, [0])
-        product(0, 0, [1])
-        product(0, 1, [1])
-        product(1, 0, [0])
-        product(1, 0, [1])
-        product(1, 1, [0])
-        product(1, 1, [1])
-        weigh(0)
-        weigh(1)
-        combine(0, [0])
-        combine(0, [1])
-        combine(1, [0])
-        combine(1, [1])
+        product(0, 0, [0, HALF], "raw_1_0")
+        product(0, 1, [0, HALF])
+        product(0, 0, [HALF, S])
+        product(0, 1, [HALF, S])
+        product(1, 0, [0, HALF])
+        product(1, 0, [HALF, S])
+        product(1, 1, [0, HALF])
+        product(1, 1, [HALF, S])
+        weigh(0, 0, HALF, None, "grouped_1_0")
+        weigh(1, 0, HALF)
+        weigh(0, HALF, S)
+        weigh(1, HALF, S)
+        combine(0, 0, HALF)
+        combine(0, HALF, S)
+        combine(1, 0, HALF)
+        combine(1, HALF, S)

@@ -49,10 +49,16 @@ def tile_picked_zmos_sig_p_kernel(tc, x_words, x_scales, hT, gT, mix, offs, out)
             src = heads[head].rearrange("(p j) c -> p j c", j=PACK)
             queue.dma_start(out=raw[head, a][:], in_=src[:, :, a * P : (a + 1) * P])
 
+        def load_whole(queue, head):
+            whole = sb.tile([P, PACK, J], F32, name="raw_%d" % head, align_bytes=64)
+            queue.dma_start(out=whole[:], in_=heads[head].rearrange("(p j) c -> p j c", j=PACK))
+            for a in range(2):
+                raw[head, a] = whole[:, :, a * P : (a + 1) * P]
+
         def load_scales(queue, q):
             queue.dma_start(
-                out=table_scales[32 * q : 32 * q + 4, :].bitcast(I32),
-                in_=x_scales[0, 4 * q : 4 * q + 4, :].bitcast(I32),
+                out=table_scales[q:P:32, :].bitcast(I32),
+                in_=x_scales[0, q:16:4, :].bitcast(I32),
             )
 
         def load_words(queue):
@@ -82,6 +88,29 @@ def tile_picked_zmos_sig_p_kernel(tc, x_words, x_scales, hT, gT, mix, offs, out)
                 scales=planes[head, a][:],
                 in_=grouped[head, a][:].rearrange("p c t -> p (c t)"),
             )
+
+        def cast_pair(head, engines):
+            pair = sb.tile([P, 2, P, PACK], BF16, name="grouped_%d" % head, align_bytes=64)
+            grouped[head] = pair
+            for a in range(2):
+                dst = pair[:, a].rearrange("p (c i) t -> p c t i", i=4)
+                src = raw[head, a].rearrange("p t (c i) -> p c t i", i=4)
+                if engines[a] == "scalar":
+                    nc.scalar.copy(dst, src)
+                else:
+                    nc.vector.tensor_copy(dst, src)
+
+        def quantize_pair(head, tag):
+            words = sb.tile([P, J], U32, name="codes_%d" % head, tag=tag, align_bytes=64)
+            plane = sb.tile([P, J], U8, name="planes_%d" % head, align_bytes=64)
+            nc.vector.quantize_mx(
+                out=words[:].bitcast(FP8X4),
+                scales=plane[:],
+                in_=grouped[head][:].rearrange("p a c t -> p (a c t)"),
+            )
+            for a in range(2):
+                codes[head, a] = words[:, a * P : (a + 1) * P]
+                planes[head, a] = plane[:, a * P : (a + 1) * P]
 
         def gather_scales(lo, hi):
             nc.vector.tensor_copy(picked_scales[:, lo:hi], table_scales[:].indirect(offsets[:, lo // 16 : hi // 16]))
@@ -131,13 +160,13 @@ def tile_picked_zmos_sig_p_kernel(tc, x_words, x_scales, hT, gT, mix, offs, out)
             (queue or nc.sync).dma_start(out=out[a * P : (a + 1) * P, lo:hi], in_=res[:])
 
         nc.vector.memset(table_scales[:].bitcast(I32), 0)
-        warm_up()
         load(nc.sync, 0, 0)
         nc.sync.dma_start(offsets[:], offs)
         load_scales(nc.sync, 0)
+        load_scales(nc.scalar, 2)
         load_scales(nc.sync, 1)
-        load_scales(nc.sync, 2)
-        load_scales(nc.sync, 3)
+        load_scales(nc.scalar, 3)
+        warm_up()
         load(nc.sync, 0, 1)
         load_words(nc.sync)
         load(nc.sync, 1, 0)

@@ -100,6 +100,12 @@ def tile_picked_zmos_sig_p_kernel(tc, x_words, x_scales, hT, gT, mix, offs, out)
                 else:
                     nc.vector.tensor_copy(dst, src)
 
+        def cast_into_pair(head, a):
+            if a == 0:
+                grouped[head] = sb.tile([P, 2, P, PACK], BF16, name="grouped_%d" % head, align_bytes=64)
+            dst = grouped[head][:, a].rearrange("p (c i) t -> p c t i", i=4)
+            nc.scalar.copy(dst, raw[head, a][:].rearrange("p t (c i) -> p c t i", i=4))
+
         def quantize_pair(head, tag):
             words = sb.tile([P, J], U32, name="codes_%d" % head, tag=tag, align_bytes=64)
             plane = sb.tile([P, J], U8, name="planes_%d" % head, align_bytes=64)
@@ -121,7 +127,7 @@ def tile_picked_zmos_sig_p_kernel(tc, x_words, x_scales, hT, gT, mix, offs, out)
             )
 
         def warm_up():
-            nc.gpsimd.memset(warm_in[:], 0.0)
+            nc.vector.memset(warm_in[:], 0.0)
             nc.scalar.activation(warm_out[:], warm_in[:], SIGMOID)
 
         def product(head, a, cuts, tag=None):
@@ -159,6 +165,7 @@ def tile_picked_zmos_sig_p_kernel(tc, x_words, x_scales, hT, gT, mix, offs, out)
             )
             (queue or nc.sync).dma_start(out=out[a * P : (a + 1) * P, lo:hi], in_=res[:])
 
+        warm_up()
         nc.vector.memset(table_scales[:].bitcast(I32), 0)
         load(nc.sync, 0, 0)
         nc.sync.dma_start(offsets[:], offs)
@@ -166,7 +173,6 @@ def tile_picked_zmos_sig_p_kernel(tc, x_words, x_scales, hT, gT, mix, offs, out)
         load_scales(nc.scalar, 2)
         load_scales(nc.sync, 1)
         load_scales(nc.scalar, 3)
-        warm_up()
         load(nc.sync, 0, 1)
         load_words(nc.sync)
         load(nc.sync, 1, 0)

@@ -26,6 +26,7 @@ def tile_picked_zmos_sig_p_kernel(tc, x_words, x_scales, hT, gT, mix, offs, out)
     with ExitStack() as ctx:
         sb = ctx.enter_context(tc.tile_pool(name="sb", bufs=1))
         ps = ctx.enter_context(tc.psum_pool(name="ps", bufs=1))
+        shared = ctx.enter_context(tc.tile_pool(name="shared", bufs=1))
 
         offsets = sb.tile([P, S // 16], U16, name="offsets")
         table_scales = sb.tile([P, T], U8, name="table_scales", align_bytes=64)
@@ -45,7 +46,10 @@ def tile_picked_zmos_sig_p_kernel(tc, x_words, x_scales, hT, gT, mix, offs, out)
         part = {}
 
         def load(queue, head, a):
-            raw[head, a] = sb.tile([P, PACK, P], F32, name="raw_%d_%d" % (head, a), align_bytes=64)
+            if (head, a) == (1, 0):
+                raw[head, a] = shared.tile([P, PACK, P], F32, name="raw_1_0", align_bytes=64, offset=7168)
+            else:
+                raw[head, a] = sb.tile([P, PACK, P], F32, name="raw_%d_%d" % (head, a), align_bytes=64)
             src = heads[head].rearrange("(p j) c -> p j c", j=PACK)
             queue.dma_start(out=raw[head, a][:], in_=src[:, :, a * P : (a + 1) * P])
 
@@ -69,7 +73,10 @@ def tile_picked_zmos_sig_p_kernel(tc, x_words, x_scales, hT, gT, mix, offs, out)
 
         def cast(head, a, engine, tag=None):
             name = "grouped_%d_%d" % (head, a)
-            grouped[head, a] = sb.tile([P, P, PACK], BF16, name=name, tag=tag or name, align_bytes=64)
+            if (head, a) == (1, 1):
+                grouped[head, a] = shared.tile([P, P, PACK], BF16, name=name, align_bytes=64, offset=8192)
+            else:
+                grouped[head, a] = sb.tile([P, P, PACK], BF16, name=name, tag=tag or name, align_bytes=64)
             dst = grouped[head, a][:].rearrange("p (c i) t -> p c t i", i=4)
             src = raw[head, a][:].rearrange("p t (c i) -> p c t i", i=4)
             if engine == "scalar":
@@ -130,13 +137,13 @@ def tile_picked_zmos_sig_p_kernel(tc, x_words, x_scales, hT, gT, mix, offs, out)
             nc.vector.memset(warm_in[:], 0.0)
             nc.scalar.activation(warm_out[:], warm_in[:], SIGMOID)
 
-        def product(head, a, cuts, tag=None):
+        def product(head, a, cuts, bank):
             if not prob:
-                every = sb.tile([P, 4, S], F32, name="prob", tag=tag or "prob", align_bytes=64)
+                every = shared.tile([P, 4, S], F32, name="prob", align_bytes=64, offset=0)
                 for i in range(4):
                     prob[i % 2, i // 2] = every[:, i, :]
             lo, hi = cuts[0], cuts[-1]
-            acc = ps.tile([P, hi - lo], F32, name="acc_%d_%d_%d" % (head, a, lo))
+            acc = ps.tile([P, hi - lo], F32, name="acc_%d_%d_%d" % (head, a, lo), tag="bank_%d" % (bank % 8))
             for c0, c1 in zip(cuts[:-1], cuts[1:]):
                 nc.tensor.matmul_mx(
                     out=acc[:, c0 - lo : c1 - lo],
@@ -183,24 +190,29 @@ def tile_picked_zmos_sig_p_kernel(tc, x_words, x_scales, hT, gT, mix, offs, out)
         cast(0, 1, "scalar")
         quantize(0, 0, "raw_0_1")
         quantize(0, 1)
-        gather_words(0, HALF)
-        gather_words(HALF, S)
+        gather_words(0, 128)
+        gather_words(128, 256)
+        gather_words(256, 384)
+        gather_words(384, S)
         cast(1, 0, "scalar")
-        cast(1, 1, "vector")
         quantize(1, 0)
-        quantize(1, 1)
-        product(0, 0, [0, HALF], "raw_1_0")
-        product(0, 1, [0, HALF])
-        product(0, 0, [HALF, S])
-        product(0, 1, [HALF, S])
-        product(1, 0, [0, HALF])
-        product(1, 0, [HALF, S])
-        product(1, 1, [0, HALF])
-        product(1, 1, [HALF, S])
+        cast(1, 1, "vector")
+        product(0, 0, [0, 128], 0)
+        product(0, 1, [0, 128], 1)
+        product(0, 0, [128, 256], 2)
+        product(0, 1, [128, 256], 3)
+        product(0, 0, [256, 384], 4)
+        product(0, 1, [256, 384], 5)
+        product(0, 0, [384, S], 6)
+        product(0, 1, [384, S], 7)
+        product(1, 0, [0, HALF], 8)
+        product(1, 0, [HALF, S], 9)
         weigh(0, 0, HALF, None, "grouped_1_0")
-        weigh(1, 0, HALF)
+        quantize(1, 1)
+        product(1, 1, [0, HALF], 10)
+        product(1, 1, [HALF, S], 11)
         weigh(0, HALF, S)
-        weigh(1, HALF, S)
+        weigh(1, 0, S)
         combine(0, 0, HALF)
         combine(0, HALF, S)
         combine(1, 0, HALF)

@@ -18,7 +18,17 @@ SIGMOID = mybir.ActivationFunctionType.Sigmoid
 
 P = 128
 PACK = 4
+BLOCK = 32
+QUADRANT = 32
+ROWS = 4
+LIST_GROUP = 16
+BANKS = 8
+PIECE = 128
 HALF = S // 2
+RUN = 4
+
+SIGMOIDS_BYTES = 2 * 2 * S * 4
+RAW_BYTES = PACK * P * 4
 
 
 def tile_picked_zmos_sig_p_kernel(tc, x_words, x_scales, hT, gT, mix, offs, out):
@@ -26,9 +36,9 @@ def tile_picked_zmos_sig_p_kernel(tc, x_words, x_scales, hT, gT, mix, offs, out)
     with ExitStack() as ctx:
         sb = ctx.enter_context(tc.tile_pool(name="sb", bufs=1))
         ps = ctx.enter_context(tc.psum_pool(name="ps", bufs=1))
-        shared = ctx.enter_context(tc.tile_pool(name="shared", bufs=1))
+        placed = ctx.enter_context(tc.tile_pool(name="placed", bufs=1))
 
-        offsets = sb.tile([P, S // 16], U16, name="offsets")
+        offsets = sb.tile([P, S // LIST_GROUP], U16, name="offsets")
         table_scales = sb.tile([P, T], U8, name="table_scales", align_bytes=64)
         table_words = sb.tile([P, T], I32, name="table_words", align_bytes=64)
         weights = sb.tile([P, 2, 2], F32, name="weights", align_bytes=64)
@@ -37,183 +47,112 @@ def tile_picked_zmos_sig_p_kernel(tc, x_words, x_scales, hT, gT, mix, offs, out)
         picked_words = sb.tile([P, S], U32, name="picked_words", align_bytes=64)
         picked_scales = sb.tile([P, S], U8, name="picked_scales", align_bytes=64)
 
-        heads = (hT, gT)
-        raw = {}
-        grouped = {}
-        codes = {}
-        planes = {}
-        prob = {}
-        part = {}
+        raw_h = [sb.tile([P, PACK, P], F32, name="raw_h%d" % a, align_bytes=64) for a in range(2)]
+        raw_g1 = sb.tile([P, PACK, P], F32, name="raw_g1", align_bytes=64)
+        rounded_h = sb.tile([P, J, PACK], BF16, name="rounded_h", align_bytes=64)
+        rounded_g0 = sb.tile([P, P, PACK], BF16, name="rounded_g0", align_bytes=64)
 
-        def load(queue, head, a):
-            if (head, a) == (1, 0):
-                raw[head, a] = shared.tile([P, PACK, P], F32, name="raw_1_0", align_bytes=64, offset=7168)
-            else:
-                raw[head, a] = sb.tile([P, PACK, P], F32, name="raw_%d_%d" % (head, a), align_bytes=64)
-            src = heads[head].rearrange("(p j) c -> p j c", j=PACK)
-            queue.dma_start(out=raw[head, a][:], in_=src[:, :, a * P : (a + 1) * P])
+        raw_g0 = placed.tile([P, PACK, P], F32, name="raw_g0", align_bytes=64, offset=SIGMOIDS_BYTES - RAW_BYTES // 2)
+        sigmoids = placed.tile([P, 2, 2, S], F32, name="sigmoids", align_bytes=64, offset=0)
+        rounded_g1 = placed.tile([P, P, PACK], BF16, name="rounded_g1", align_bytes=64, offset=SIGMOIDS_BYTES)
 
-        def load_whole(queue, head):
-            whole = sb.tile([P, PACK, J], F32, name="raw_%d" % head, align_bytes=64)
-            queue.dma_start(out=whole[:], in_=heads[head].rearrange("(p j) c -> p j c", j=PACK))
-            for a in range(2):
-                raw[head, a] = whole[:, :, a * P : (a + 1) * P]
+        weighted = sb.tile([P, 2, S], F32, name="weighted", align_bytes=64)
+        stationary = {}
+        products = []
 
-        def load_scales(queue, q):
+        def load_tile(raw, head, a):
+            rows = head.rearrange("(p j) c -> p j c", j=PACK)
+            nc.sync.dma_start(out=raw[:], in_=rows[:, :, a * P : (a + 1) * P])
+
+        def load_scales(queue, r):
             queue.dma_start(
-                out=table_scales[q:P:32, :].bitcast(I32),
-                in_=x_scales[0, q:16:4, :].bitcast(I32),
+                out=table_scales[r:P:QUADRANT, :].bitcast(I32),
+                in_=x_scales[0, r : K // BLOCK : ROWS, :].bitcast(I32),
             )
 
-        def load_words(queue):
-            queue.dma_start(out=table_words[:], in_=x_words[0].rearrange("p n t -> p (n t)").bitcast(I32))
+        def round_tile(copy, rounded, raw):
+            copy(
+                rounded.rearrange("p (c i) j -> p c j i", i=RUN),
+                raw[:].rearrange("p j (c i) -> p c j i", i=RUN),
+            )
 
-        def load_mix(queue):
-            queue.dma_start(out=weights[:], in_=mix.rearrange("(a p) c -> p a c", p=P))
-
-        def cast(head, a, engine, tag=None):
-            name = "grouped_%d_%d" % (head, a)
-            if (head, a) == (1, 1):
-                grouped[head, a] = shared.tile([P, P, PACK], BF16, name=name, align_bytes=64, offset=8192)
-            else:
-                grouped[head, a] = sb.tile([P, P, PACK], BF16, name=name, tag=tag or name, align_bytes=64)
-            dst = grouped[head, a][:].rearrange("p (c i) t -> p c t i", i=4)
-            src = raw[head, a][:].rearrange("p t (c i) -> p c t i", i=4)
-            if engine == "scalar":
-                nc.scalar.copy(dst, src)
-            elif engine == "gpsimd":
-                nc.gpsimd.tensor_copy(dst, src)
-            else:
-                nc.vector.tensor_copy(dst, src)
-
-        def quantize(head, a, tag=None):
-            name = "codes_%d_%d" % (head, a)
-            codes[head, a] = sb.tile([P, P], U32, name=name, tag=tag or name, align_bytes=64)
-            planes[head, a] = sb.tile([P, P], U8, name="planes_%d_%d" % (head, a), align_bytes=64)
+        def quantize(head, tiles, rounded):
+            width = len(tiles) * P
+            words = sb.tile([P, width], U32, name="words_%d_%d" % (head, tiles[0]), align_bytes=64)
+            scales = sb.tile([P, width], U8, name="scales_%d_%d" % (head, tiles[0]), align_bytes=64)
             nc.vector.quantize_mx(
-                out=codes[head, a][:].bitcast(FP8X4),
-                scales=planes[head, a][:],
-                in_=grouped[head, a][:].rearrange("p c t -> p (c t)"),
+                out=words[:].bitcast(FP8X4), scales=scales[:], in_=rounded[:].rearrange("p c j -> p (c j)")
             )
+            for n, a in enumerate(tiles):
+                stationary[head, a] = (words[:, n * P : (n + 1) * P], scales[:, n * P : (n + 1) * P])
 
-        def cast_pair(head, engines):
-            pair = sb.tile([P, 2, P, PACK], BF16, name="grouped_%d" % head, align_bytes=64)
-            grouped[head] = pair
-            for a in range(2):
-                dst = pair[:, a].rearrange("p (c i) t -> p c t i", i=4)
-                src = raw[head, a].rearrange("p t (c i) -> p c t i", i=4)
-                if engines[a] == "scalar":
-                    nc.scalar.copy(dst, src)
-                else:
-                    nc.vector.tensor_copy(dst, src)
-
-        def cast_into_pair(head, a):
-            if a == 0:
-                grouped[head] = sb.tile([P, 2, P, PACK], BF16, name="grouped_%d" % head, align_bytes=64)
-            dst = grouped[head][:, a].rearrange("p (c i) t -> p c t i", i=4)
-            nc.scalar.copy(dst, raw[head, a][:].rearrange("p t (c i) -> p c t i", i=4))
-
-        def quantize_pair(head, tag):
-            words = sb.tile([P, J], U32, name="codes_%d" % head, tag=tag, align_bytes=64)
-            plane = sb.tile([P, J], U8, name="planes_%d" % head, align_bytes=64)
-            nc.vector.quantize_mx(
-                out=words[:].bitcast(FP8X4),
-                scales=plane[:],
-                in_=grouped[head][:].rearrange("p a c t -> p (a c t)"),
+        def product(head, a, lo, hi):
+            n = len(products)
+            acc = ps.tile([P, hi - lo], F32, name="acc_%d" % n, tag="bank_%d" % (n % BANKS))
+            products.append(acc)
+            words, scales = stationary[head, a]
+            nc.tensor.matmul_mx(
+                out=acc[:],
+                lhsT=words.bitcast(FP8X4),
+                lhsT_scale=scales,
+                rhs=picked_words[:, lo:hi].bitcast(FP8X4),
+                rhs_scale=picked_scales[:, lo:hi],
+                start=True,
+                stop=True,
             )
-            for a in range(2):
-                codes[head, a] = words[:, a * P : (a + 1) * P]
-                planes[head, a] = plane[:, a * P : (a + 1) * P]
+            nc.scalar.activation(sigmoids[:, a, head, lo:hi], acc[:], SIGMOID)
 
-        def gather_scales(lo, hi):
-            nc.vector.tensor_copy(picked_scales[:, lo:hi], table_scales[:].indirect(offsets[:, lo // 16 : hi // 16]))
+        def weigh(a, lo, hi):
+            nc.vector.tensor_scalar(weighted[:, a, lo:hi], sigmoids[:, a, 0, lo:hi], weights[:, a, 0:1], None, MULT)
 
-        def gather_words(lo, hi):
-            nc.vector.tensor_copy(
-                picked_words[:, lo:hi], table_words[:].bitcast(U32).indirect(offsets[:, lo // 16 : hi // 16])
-            )
-
-        def warm_up():
-            nc.vector.memset(warm_in[:], 0.0)
-            nc.scalar.activation(warm_out[:], warm_in[:], SIGMOID)
-
-        def product(head, a, cuts, bank):
-            if not prob:
-                every = shared.tile([P, 4, S], F32, name="prob", align_bytes=64, offset=0)
-                for i in range(4):
-                    prob[i % 2, i // 2] = every[:, i, :]
-            lo, hi = cuts[0], cuts[-1]
-            acc = ps.tile([P, hi - lo], F32, name="acc_%d_%d_%d" % (head, a, lo), tag="bank_%d" % (bank % 8))
-            for c0, c1 in zip(cuts[:-1], cuts[1:]):
-                nc.tensor.matmul_mx(
-                    out=acc[:, c0 - lo : c1 - lo],
-                    lhsT=codes[head, a][:].bitcast(FP8X4),
-                    lhsT_scale=planes[head, a][:],
-                    rhs=picked_words[:, c0:c1].bitcast(FP8X4),
-                    rhs_scale=picked_scales[:, c0:c1],
-                    start=True,
-                    stop=True,
-                )
-            nc.scalar.activation(prob[head, a][:, lo:hi], acc[:], SIGMOID)
-
-        def weigh(a, lo, hi, engine=None, tag=None):
-            if a not in part:
-                both = sb.tile([P, 2, S], F32, name="part", tag=tag or "part", align_bytes=64)
-                part[0] = both[:, 0, :]
-                part[1] = both[:, 1, :]
-            (engine or nc.vector).tensor_scalar(
-                part[a][:, lo:hi], prob[0, a][:, lo:hi], weights[:, a, 0:1], None, MULT
-            )
-
-        def combine(a, lo, hi, queue=None):
-            res = sb.tile([P, hi - lo], F32, name="res_%d_%d" % (a, lo))
+        def mix_and_store(a, lo, hi):
+            result = sb.tile([P, hi - lo], F32, name="result_%d_%d" % (a, lo))
             nc.vector.scalar_tensor_tensor(
-                res[:], prob[1, a][:, lo:hi], weights[:, a, 1:2], part[a][:, lo:hi], MULT, ADD
+                result[:], sigmoids[:, a, 1, lo:hi], weights[:, a, 1:2], weighted[:, a, lo:hi], MULT, ADD
             )
-            (queue or nc.sync).dma_start(out=out[a * P : (a + 1) * P, lo:hi], in_=res[:])
+            nc.sync.dma_start(out=out[a * P : (a + 1) * P, lo:hi], in_=result[:])
 
-        warm_up()
-        nc.vector.memset(table_scales[:].bitcast(I32), 0)
-        load(nc.sync, 0, 0)
+        nc.vector.memset(warm_in[:], 0.0)
+        nc.scalar.activation(warm_out[:], warm_in[:], SIGMOID)
+
+        nc.gpsimd.memset(table_scales[:].bitcast(I32), 0)
+
+        load_tile(raw_h[0], hT, 0)
         nc.sync.dma_start(offsets[:], offs)
-        load_scales(nc.sync, 0)
-        load_scales(nc.scalar, 2)
-        load_scales(nc.sync, 1)
-        load_scales(nc.scalar, 3)
-        load(nc.sync, 0, 1)
-        load_words(nc.sync)
-        load(nc.sync, 1, 0)
-        load(nc.sync, 1, 1)
-        load_mix(nc.sync)
-        cast(0, 0, "scalar")
-        gather_scales(0, S)
-        cast(0, 1, "scalar")
-        quantize(0, 0, "raw_0_1")
-        quantize(0, 1)
-        gather_words(0, 128)
-        gather_words(128, 256)
-        gather_words(256, 384)
-        gather_words(384, S)
-        cast(1, 0, "scalar")
-        quantize(1, 0)
-        cast(1, 1, "vector")
-        product(0, 0, [0, 128], 0)
-        product(0, 1, [0, 128], 1)
-        product(0, 0, [128, 256], 2)
-        product(0, 1, [128, 256], 3)
-        product(0, 0, [256, 384], 4)
-        product(0, 1, [256, 384], 5)
-        product(0, 0, [384, S], 6)
-        product(0, 1, [384, S], 7)
-        product(1, 0, [0, HALF], 8)
-        product(1, 0, [HALF, S], 9)
-        weigh(0, 0, HALF, None, "grouped_1_0")
-        quantize(1, 1)
-        product(1, 1, [0, HALF], 10)
-        product(1, 1, [HALF, S], 11)
+        for r in range(ROWS // 2):
+            load_scales(nc.sync, r)
+            load_scales(nc.scalar, ROWS // 2 + r)
+        load_tile(raw_h[1], hT, 1)
+        nc.sync.dma_start(out=table_words[:], in_=x_words[0].rearrange("p n t -> p (n t)").bitcast(I32))
+        load_tile(raw_g0, gT, 0)
+        load_tile(raw_g1, gT, 1)
+        nc.sync.dma_start(out=weights[:], in_=mix.rearrange("(a p) c -> p a c", p=P))
+
+        round_tile(nc.scalar.copy, rounded_h[:, :P], raw_h[0])
+        nc.vector.tensor_copy(picked_scales[:], table_scales[:].indirect(offsets[:]))
+        round_tile(nc.scalar.copy, rounded_h[:, P:], raw_h[1])
+        quantize(0, (0, 1), rounded_h)
+        for lo in range(0, S, PIECE):
+            columns = offsets[:, lo // LIST_GROUP : (lo + PIECE) // LIST_GROUP]
+            nc.vector.tensor_copy(picked_words[:, lo : lo + PIECE], table_words[:].bitcast(U32).indirect(columns))
+
+        round_tile(nc.scalar.copy, rounded_g0[:], raw_g0)
+        quantize(1, (0,), rounded_g0)
+        round_tile(nc.vector.tensor_copy, rounded_g1[:], raw_g1)
+
+        for lo in range(0, S, PIECE):
+            for a in range(2):
+                product(0, a, lo, lo + PIECE)
+        for lo in range(0, S, HALF):
+            product(1, 0, lo, lo + HALF)
+
+        weigh(0, 0, HALF)
+        quantize(1, (1,), rounded_g1)
+        for lo in range(0, S, HALF):
+            product(1, 1, lo, lo + HALF)
+
         weigh(0, HALF, S)
         weigh(1, 0, S)
-        combine(0, 0, HALF)
-        combine(0, HALF, S)
-        combine(1, 0, HALF)
-        combine(1, HALF, S)
+        for a in range(2):
+            for lo in range(0, S, HALF):
+                mix_and_store(a, lo, lo + HALF)

@@ -47,9 +47,9 @@ def tile_picked_zmos_sig_p_kernel(tc, x_words, x_scales, hT, gT, mix, offs, out)
         picked_words = sb.tile([P, S], U32, name="picked_words", align_bytes=64)
         picked_scales = sb.tile([P, S], U8, name="picked_scales", align_bytes=64)
 
-        raw_h = [sb.tile([P, PACK, P], F32, name="raw_h%d" % a, align_bytes=64) for a in range(2)]
+        raw_h = sb.tile([P, PACK, J], F32, name="raw_h", align_bytes=64)
         raw_g1 = sb.tile([P, PACK, P], F32, name="raw_g1", align_bytes=64)
-        rounded_h = sb.tile([P, J, PACK], BF16, name="rounded_h", align_bytes=64)
+        rounded_h = [sb.tile([P, P, PACK], BF16, name="rounded_h%d" % a, align_bytes=64) for a in range(2)]
         rounded_g0 = sb.tile([P, P, PACK], BF16, name="rounded_g0", align_bytes=64)
 
         raw_g0 = placed.tile([P, PACK, P], F32, name="raw_g0", align_bytes=64, offset=SIGMOIDS_BYTES - RAW_BYTES // 2)
@@ -73,7 +73,7 @@ def tile_picked_zmos_sig_p_kernel(tc, x_words, x_scales, hT, gT, mix, offs, out)
         def round_tile(copy, rounded, raw):
             copy(
                 rounded.rearrange("p (c i) j -> p c j i", i=RUN),
-                raw[:].rearrange("p j (c i) -> p c j i", i=RUN),
+                raw.rearrange("p j (c i) -> p c j i", i=RUN),
             )
 
         def quantize(head, tiles, rounded):
@@ -117,28 +117,29 @@ def tile_picked_zmos_sig_p_kernel(tc, x_words, x_scales, hT, gT, mix, offs, out)
 
         nc.gpsimd.memset(table_scales[:].bitcast(I32), 0)
 
-        load_tile(raw_h[0], hT, 0)
+        h_rows = hT.rearrange("(p j) c -> p j c", j=PACK)
+        nc.sync.dma_start(out=raw_h[:, : PACK // 2, :], in_=h_rows[:, : PACK // 2, :])
         nc.sync.dma_start(offsets[:], offs)
         for r in range(ROWS // 2):
             load_scales(nc.sync, r)
             load_scales(nc.scalar, ROWS // 2 + r)
-        load_tile(raw_h[1], hT, 1)
+        nc.sync.dma_start(out=raw_h[:, PACK // 2 :, :], in_=h_rows[:, PACK // 2 :, :])
         nc.sync.dma_start(out=table_words[:], in_=x_words[0].rearrange("p n t -> p (n t)").bitcast(I32))
         load_tile(raw_g0, gT, 0)
         load_tile(raw_g1, gT, 1)
         nc.sync.dma_start(out=weights[:], in_=mix.rearrange("(a p) c -> p a c", p=P))
 
-        round_tile(nc.scalar.copy, rounded_h[:, :P], raw_h[0])
         nc.vector.tensor_copy(picked_scales[:], table_scales[:].indirect(offsets[:]))
-        round_tile(nc.scalar.copy, rounded_h[:, P:], raw_h[1])
-        quantize(0, (0, 1), rounded_h)
+        for a in range(2):
+            round_tile(nc.scalar.copy, rounded_h[a][:], raw_h[:, :, a * P : (a + 1) * P])
+            quantize(0, (a,), rounded_h[a])
         for lo in range(0, S, PIECE):
             columns = offsets[:, lo // LIST_GROUP : (lo + PIECE) // LIST_GROUP]
             nc.vector.tensor_copy(picked_words[:, lo : lo + PIECE], table_words[:].bitcast(U32).indirect(columns))
 
-        round_tile(nc.scalar.copy, rounded_g0[:], raw_g0)
+        round_tile(nc.scalar.copy, rounded_g0[:], raw_g0[:])
         quantize(1, (0,), rounded_g0)
-        round_tile(nc.vector.tensor_copy, rounded_g1[:], raw_g1)
+        round_tile(nc.vector.tensor_copy, rounded_g1[:], raw_g1[:])
 
         for lo in range(0, S, PIECE):
             for a in range(2):

@@ -27,8 +27,8 @@ PIECE = 128
 HALF = S // 2
 RUN = 4
 
-SIGMOIDS_BYTES = 2 * 2 * S * 4
-RAW_BYTES = PACK * P * 4
+RAW = PACK * P
+SHARE = P // 2
 
 
 def tile_picked_zmos_sig_p_kernel(tc, x_words, x_scales, hT, gT, mix, offs, out):
@@ -48,21 +48,31 @@ def tile_picked_zmos_sig_p_kernel(tc, x_words, x_scales, hT, gT, mix, offs, out)
         picked_scales = sb.tile([P, S], U8, name="picked_scales", align_bytes=64)
 
         raw_h = sb.tile([P, PACK, J], F32, name="raw_h", align_bytes=64)
-        raw_g1 = sb.tile([P, PACK, P], F32, name="raw_g1", align_bytes=64)
+        raw_g1 = placed.tile([P, PACK, P], F32, name="raw_g1", align_bytes=64, offset=0)
         rounded_h = [sb.tile([P, P, PACK], BF16, name="rounded_h%d" % a, align_bytes=64) for a in range(2)]
         rounded_g0 = sb.tile([P, P, PACK], BF16, name="rounded_g0", align_bytes=64)
 
-        raw_g0 = placed.tile([P, PACK, P], F32, name="raw_g0", align_bytes=64, offset=SIGMOIDS_BYTES - RAW_BYTES // 2)
-        sigmoids = placed.tile([P, 2, 2, S], F32, name="sigmoids", align_bytes=64, offset=0)
-        rounded_g1 = placed.tile([P, P, PACK], BF16, name="rounded_g1", align_bytes=64, offset=SIGMOIDS_BYTES)
+        g0_at = RAW // 2 - SHARE
+        sigmoids_at = g0_at + RAW - SHARE
+        shared = sb.tile([P, sigmoids_at + 2 * S], F32, name="shared", align_bytes=64)
+        raw_g0 = shared[:, g0_at : g0_at + RAW].rearrange("p (j c) -> p j c", j=PACK)
+        rounded_g1 = shared[:, : RAW // 2].bitcast(BF16).rearrange("p (c j) -> p c j", j=PACK)
+        sigmoids_h = shared[:, sigmoids_at:].rearrange("p (a s) -> p a s", a=2)
+        sigmoids_g = sb.tile([P, 2, S], F32, name="sigmoids_g", align_bytes=64)
 
-        weighted = sb.tile([P, 2, S], F32, name="weighted", align_bytes=64)
+        weighted = placed.tile([P, 2, S], F32, name="weighted", align_bytes=64, offset=0)
         stationary = {}
+        for head in range(2):
+            for a in range(2):
+                stationary[head, a] = (
+                    sb.tile([P, P], U32, name="words_%d_%d" % (head, a), align_bytes=64)[:],
+                    sb.tile([P, P], U8, name="scales_%d_%d" % (head, a), align_bytes=64)[:],
+                )
         products = []
 
         def load_tile(raw, head, a):
             rows = head.rearrange("(p j) c -> p j c", j=PACK)
-            nc.sync.dma_start(out=raw[:], in_=rows[:, :, a * P : (a + 1) * P])
+            nc.sync.dma_start(out=raw, in_=rows[:, :, a * P : (a + 1) * P])
 
         def load_scales(queue, r):
             queue.dma_start(
@@ -76,39 +86,39 @@ def tile_picked_zmos_sig_p_kernel(tc, x_words, x_scales, hT, gT, mix, offs, out)
                 raw.rearrange("p j (c i) -> p c j i", i=RUN),
             )
 
-        def quantize(head, tiles, rounded):
-            width = len(tiles) * P
-            words = sb.tile([P, width], U32, name="words_%d_%d" % (head, tiles[0]), align_bytes=64)
-            scales = sb.tile([P, width], U8, name="scales_%d_%d" % (head, tiles[0]), align_bytes=64)
-            nc.vector.quantize_mx(
-                out=words[:].bitcast(FP8X4), scales=scales[:], in_=rounded[:].rearrange("p c j -> p (c j)")
-            )
-            for n, a in enumerate(tiles):
-                stationary[head, a] = (words[:, n * P : (n + 1) * P], scales[:, n * P : (n + 1) * P])
-
-        def product(head, a, lo, hi):
-            n = len(products)
-            acc = ps.tile([P, hi - lo], F32, name="acc_%d" % n, tag="bank_%d" % (n % BANKS))
-            products.append(acc)
+        def quantize(head, a, rounded, lo, hi):
             words, scales = stationary[head, a]
-            nc.tensor.matmul_mx(
-                out=acc[:],
-                lhsT=words.bitcast(FP8X4),
-                lhsT_scale=scales,
-                rhs=picked_words[:, lo:hi].bitcast(FP8X4),
-                rhs_scale=picked_scales[:, lo:hi],
-                start=True,
-                stop=True,
+            nc.vector.quantize_mx(
+                out=words[:, lo:hi].bitcast(FP8X4),
+                scales=scales[:, lo:hi],
+                in_=rounded[:, lo:hi, :].rearrange("p c j -> p (c j)"),
             )
-            nc.scalar.activation(sigmoids[:, a, head, lo:hi], acc[:], SIGMOID)
+
+        def product(head, tiles, lo, hi):
+            n = len(products)
+            acc = ps.tile([P, len(tiles), hi - lo], F32, name="acc_%d" % n, tag="bank_%d" % (n % BANKS))
+            products.append(acc)
+            for i, a in enumerate(tiles):
+                words, scales = stationary[head, a]
+                nc.tensor.matmul_mx(
+                    out=acc[:, i, :],
+                    lhsT=words.bitcast(FP8X4),
+                    lhsT_scale=scales,
+                    rhs=picked_words[:, lo:hi].bitcast(FP8X4),
+                    rhs_scale=picked_scales[:, lo:hi],
+                    start=True,
+                    stop=True,
+                )
+            sigmoids = (sigmoids_h, sigmoids_g)[head]
+            nc.scalar.activation(sigmoids[:, tiles[0] : tiles[-1] + 1, lo:hi], acc[:], SIGMOID)
 
         def weigh(a, lo, hi):
-            nc.vector.tensor_scalar(weighted[:, a, lo:hi], sigmoids[:, a, 0, lo:hi], weights[:, a, 0:1], None, MULT)
+            nc.vector.tensor_scalar(weighted[:, a, lo:hi], sigmoids_h[:, a, lo:hi], weights[:, a, 0:1], None, MULT)
 
         def mix_and_store(a, lo, hi):
             result = sb.tile([P, hi - lo], F32, name="result_%d_%d" % (a, lo))
             nc.vector.scalar_tensor_tensor(
-                result[:], sigmoids[:, a, 1, lo:hi], weights[:, a, 1:2], weighted[:, a, lo:hi], MULT, ADD
+                result[:], sigmoids_g[:, a, lo:hi], weights[:, a, 1:2], weighted[:, a, lo:hi], MULT, ADD
             )
             nc.sync.dma_start(out=out[a * P : (a + 1) * P, lo:hi], in_=result[:])
 
@@ -126,34 +136,36 @@ def tile_picked_zmos_sig_p_kernel(tc, x_words, x_scales, hT, gT, mix, offs, out)
         nc.sync.dma_start(out=raw_h[:, PACK // 2 :, :], in_=h_rows[:, PACK // 2 :, :])
         nc.sync.dma_start(out=table_words[:], in_=x_words[0].rearrange("p n t -> p (n t)").bitcast(I32))
         load_tile(raw_g0, gT, 0)
-        load_tile(raw_g1, gT, 1)
+        load_tile(raw_g1[:], gT, 1)
         nc.sync.dma_start(out=weights[:], in_=mix.rearrange("(a p) c -> p a c", p=P))
 
         nc.vector.tensor_copy(picked_scales[:], table_scales[:].indirect(offsets[:]))
         for a in range(2):
             round_tile(nc.scalar.copy, rounded_h[a][:], raw_h[:, :, a * P : (a + 1) * P])
-            quantize(0, (a,), rounded_h[a])
+            quantize(0, a, rounded_h[a], 0, P)
         for lo in range(0, S, PIECE):
             columns = offsets[:, lo // LIST_GROUP : (lo + PIECE) // LIST_GROUP]
             nc.vector.tensor_copy(picked_words[:, lo : lo + PIECE], table_words[:].bitcast(U32).indirect(columns))
 
-        round_tile(nc.scalar.copy, rounded_g0[:], raw_g0[:])
-        quantize(1, (0,), rounded_g0)
-        round_tile(nc.vector.tensor_copy, rounded_g1[:], raw_g1[:])
+        for lo in (SHARE, 0):
+            round_tile(nc.scalar.copy, rounded_g0[:, lo : lo + SHARE, :], raw_g0[:, :, lo : lo + SHARE])
+        round_tile(nc.vector.tensor_copy, rounded_g1[:, :SHARE, :], raw_g1[:, :, :SHARE])
+        quantize(1, 0, rounded_g0, 0, P)
+        round_tile(nc.vector.tensor_copy, rounded_g1[:, SHARE:, :], raw_g1[:, :, SHARE:])
+        for lo in (0, SHARE):
+            quantize(1, 1, rounded_g1, lo, lo + SHARE)
 
         for lo in range(0, S, PIECE):
+            product(0, (0, 1), lo, lo + PIECE)
+        for lo in range(0, S, HALF):
+            product(1, (0,), lo, lo + HALF)
+
+        for lo in range(0, S, HALF):
+            product(1, (1,), lo, lo + HALF)
+
+        for lo in range(0, S, HALF):
             for a in range(2):
-                product(0, a, lo, lo + PIECE)
-        for lo in range(0, S, HALF):
-            product(1, 0, lo, lo + HALF)
-
-        weigh(0, 0, HALF)
-        quantize(1, (1,), rounded_g1)
-        for lo in range(0, S, HALF):
-            product(1, 1, lo, lo + HALF)
-
-        weigh(0, HALF, S)
-        weigh(1, 0, S)
+                weigh(a, lo, lo + HALF)
         for a in range(2):
             for lo in range(0, S, HALF):
                 mix_and_store(a, lo, lo + HALF)

@@ -36,7 +36,6 @@ def tile_picked_zmos_sig_p_kernel(tc, x_words, x_scales, hT, gT, mix, offs, out)
     with ExitStack() as ctx:
         sb = ctx.enter_context(tc.tile_pool(name="sb", bufs=1))
         ps = ctx.enter_context(tc.psum_pool(name="ps", bufs=1))
-        placed = ctx.enter_context(tc.tile_pool(name="placed", bufs=1))
 
         offsets = sb.tile([P, S // LIST_GROUP], U16, name="offsets")
         table_scales = sb.tile([P, T], U8, name="table_scales", align_bytes=64)
@@ -48,19 +47,40 @@ def tile_picked_zmos_sig_p_kernel(tc, x_words, x_scales, hT, gT, mix, offs, out)
         picked_scales = sb.tile([P, S], U8, name="picked_scales", align_bytes=64)
 
         raw_h = sb.tile([P, PACK, J], F32, name="raw_h", align_bytes=64)
-        raw_g1 = placed.tile([P, PACK, P], F32, name="raw_g1", align_bytes=64, offset=0)
         rounded_h = [sb.tile([P, P, PACK], BF16, name="rounded_h%d" % a, align_bytes=64) for a in range(2)]
-        rounded_g0 = sb.tile([P, P, PACK], BF16, name="rounded_g0", align_bytes=64)
+        rounded_first = sb.tile([P, P, PACK], BF16, name="rounded_first", align_bytes=64)
 
-        g0_at = RAW // 2 - SHARE
-        sigmoids_at = g0_at + RAW - SHARE
-        shared = sb.tile([P, sigmoids_at + 2 * S], F32, name="shared", align_bytes=64)
-        raw_g0 = shared[:, g0_at : g0_at + RAW].rearrange("p (j c) -> p j c", j=PACK)
-        rounded_g1 = shared[:, : RAW // 2].bitcast(BF16).rearrange("p (c j) -> p c j", j=PACK)
-        sigmoids_h = shared[:, sigmoids_at:].rearrange("p (a s) -> p a s", a=2)
+        shared = sb.tile([P, 4 * PACK, J], F32, name="shared", align_bytes=64)
+        flat = shared[:].rearrange("p r c -> p (r c)")
+        raw_g = shared[:, PACK : 2 * PACK, :]
+        g_at = PACK * J
+        last_at = 2 * PACK * J - SHARE
+        rounded_last = flat[:, last_at : last_at + RAW // 2].bitcast(BF16).rearrange("p (c j) -> p c j", j=PACK)
+        by_tile = shared[:, : 2 * PACK, P:].rearrange("p (a r) (u e) -> p a r u e", a=2, u=2)
+        late_at = (2 * PACK + 1) * J
+        piece_out = [
+            by_tile[:, :, 0:2, 0, :],
+            by_tile[:, :, 0:2, 1, :],
+            by_tile[:, :, 2, :, :],
+            flat[:, late_at : late_at + 2 * PIECE].rearrange("p (a u e) -> p a u e", a=2, u=2),
+        ]
+
+        def two_runs(first, second):
+            step = second - first
+            return flat[:, first : first + 2 * step].rearrange("p (r s) -> p r s", r=2)[:, :, :PIECE]
+
+        sigmoids_h = {}
+        for a in range(2):
+            sigmoids_h[a, 0] = by_tile[:, a, 0:2].rearrange("p r u e -> p u r e")
+            sigmoids_h[a, HALF] = two_runs((a * PACK + 2) * J + P, late_at + a * PIECE).rearrange("p r (u e) -> p r u e", u=2)
         sigmoids_g = sb.tile([P, 2, S], F32, name="sigmoids_g", align_bytes=64)
-
-        weighted = placed.tile([P, 2, S], F32, name="weighted", align_bytes=64, offset=0)
+        weighted_late = sb.tile([P, 2, 2, PIECE], F32, name="weighted_late", align_bytes=64)
+        weighted = {
+            (1, 0): raw_g[:, 0:2, :P],
+            (0, 0): raw_g[:, 2:4, :P],
+            (1, HALF): weighted_late[:, 1],
+            (0, HALF): weighted_late[:, 0],
+        }
         stationary = {}
         for head in range(2):
             for a in range(2):
@@ -69,10 +89,6 @@ def tile_picked_zmos_sig_p_kernel(tc, x_words, x_scales, hT, gT, mix, offs, out)
                     sb.tile([P, P], U8, name="scales_%d_%d" % (head, a), align_bytes=64)[:],
                 )
         products = []
-
-        def load_tile(raw, head, a):
-            rows = head.rearrange("(p j) c -> p j c", j=PACK)
-            nc.sync.dma_start(out=raw, in_=rows[:, :, a * P : (a + 1) * P])
 
         def load_scales(queue, r):
             queue.dma_start(
@@ -91,10 +107,10 @@ def tile_picked_zmos_sig_p_kernel(tc, x_words, x_scales, hT, gT, mix, offs, out)
             nc.vector.quantize_mx(
                 out=words[:, lo:hi].bitcast(FP8X4),
                 scales=scales[:, lo:hi],
-                in_=rounded[:, lo:hi, :].rearrange("p c j -> p (c j)"),
+                in_=rounded.rearrange("p c j -> p (c j)"),
             )
 
-        def product(head, tiles, lo, hi):
+        def product(head, tiles, lo, hi, sigmoids):
             n = len(products)
             acc = ps.tile([P, len(tiles), hi - lo], F32, name="acc_%d" % n, tag="bank_%d" % (n % BANKS))
             products.append(acc)
@@ -109,18 +125,28 @@ def tile_picked_zmos_sig_p_kernel(tc, x_words, x_scales, hT, gT, mix, offs, out)
                     start=True,
                     stop=True,
                 )
-            sigmoids = (sigmoids_h, sigmoids_g)[head]
-            nc.scalar.activation(sigmoids[:, tiles[0] : tiles[-1] + 1, lo:hi], acc[:], SIGMOID)
+            nc.scalar.activation(sigmoids, acc[:].rearrange("p a (r e) -> p a r e", e=SHARE), SIGMOID)
 
-        def weigh(a, lo, hi):
-            nc.vector.tensor_scalar(weighted[:, a, lo:hi], sigmoids_h[:, a, lo:hi], weights[:, a, 0:1], None, MULT)
-
-        def mix_and_store(a, lo, hi):
-            result = sb.tile([P, hi - lo], F32, name="result_%d_%d" % (a, lo))
-            nc.vector.scalar_tensor_tensor(
-                result[:], sigmoids_g[:, a, lo:hi], weights[:, a, 1:2], weighted[:, a, lo:hi], MULT, ADD
+        def weigh(a, lo):
+            nc.vector.tensor_scalar(
+                weighted[a, lo].rearrange("p r (u e) -> p r u e", e=SHARE),
+                sigmoids_h[a, lo],
+                weights[:, a, 0:1],
+                None,
+                MULT,
             )
-            nc.sync.dma_start(out=out[a * P : (a + 1) * P, lo:hi], in_=result[:])
+
+        def mix_and_store(a, lo):
+            result = sb.tile([P, HALF], F32, name="result_%d_%d" % (a, lo))
+            nc.vector.scalar_tensor_tensor(
+                result[:].rearrange("p (r s) -> p r s", r=2),
+                sigmoids_g[:, a, lo : lo + HALF].rearrange("p (r s) -> p r s", r=2),
+                weights[:, a, 1:2],
+                weighted[a, lo],
+                MULT,
+                ADD,
+            )
+            nc.sync.dma_start(out=out[a * P : (a + 1) * P, lo : lo + HALF], in_=result[:])
 
         nc.vector.memset(warm_in[:], 0.0)
         nc.scalar.activation(warm_out[:], warm_in[:], SIGMOID)
@@ -135,37 +161,36 @@ def tile_picked_zmos_sig_p_kernel(tc, x_words, x_scales, hT, gT, mix, offs, out)
             load_scales(nc.scalar, ROWS // 2 + r)
         nc.sync.dma_start(out=raw_h[:, PACK // 2 :, :], in_=h_rows[:, PACK // 2 :, :])
         nc.sync.dma_start(out=table_words[:], in_=x_words[0].rearrange("p n t -> p (n t)").bitcast(I32))
-        load_tile(raw_g0, gT, 0)
-        load_tile(raw_g1[:], gT, 1)
+        g_rows = gT.rearrange("(p j) c -> p (j c)", j=PACK)
+        nc.sync.dma_start(out=flat[:, g_at + P : g_at + PACK * J], in_=g_rows[:, P:])
+        nc.sync.dma_start(out=flat[:, g_at : g_at + P], in_=g_rows[:, :P])
         nc.sync.dma_start(out=weights[:], in_=mix.rearrange("(a p) c -> p a c", p=P))
 
         nc.vector.tensor_copy(picked_scales[:], table_scales[:].indirect(offsets[:]))
         for a in range(2):
             round_tile(nc.scalar.copy, rounded_h[a][:], raw_h[:, :, a * P : (a + 1) * P])
-            quantize(0, a, rounded_h[a], 0, P)
+            quantize(0, a, rounded_h[a][:], 0, P)
         for lo in range(0, S, PIECE):
             columns = offsets[:, lo // LIST_GROUP : (lo + PIECE) // LIST_GROUP]
             nc.vector.tensor_copy(picked_words[:, lo : lo + PIECE], table_words[:].bitcast(U32).indirect(columns))
 
-        for lo in (SHARE, 0):
-            round_tile(nc.scalar.copy, rounded_g0[:, lo : lo + SHARE, :], raw_g0[:, :, lo : lo + SHARE])
-        round_tile(nc.vector.tensor_copy, rounded_g1[:, :SHARE, :], raw_g1[:, :, :SHARE])
-        quantize(1, 0, rounded_g0, 0, P)
-        round_tile(nc.vector.tensor_copy, rounded_g1[:, SHARE:, :], raw_g1[:, :, SHARE:])
         for lo in (0, SHARE):
-            quantize(1, 1, rounded_g1, lo, lo + SHARE)
+            round_tile(nc.scalar.copy, rounded_first[:, lo : lo + SHARE, :], raw_g[:, :, P + lo : P + lo + SHARE])
+        round_tile(nc.vector.tensor_copy, rounded_last[:, SHARE:, :], raw_g[:, :, SHARE:P])
+        quantize(1, 1, rounded_first[:], 0, P)
+        round_tile(nc.vector.tensor_copy, rounded_last[:, :SHARE, :], raw_g[:, :, :SHARE])
+        quantize(1, 0, rounded_last[:, SHARE:, :], SHARE, P)
+        quantize(1, 0, rounded_last[:, :SHARE, :], 0, SHARE)
 
-        for lo in range(0, S, PIECE):
-            product(0, (0, 1), lo, lo + PIECE)
-        for lo in range(0, S, HALF):
-            product(1, (0,), lo, lo + HALF)
-
-        for lo in range(0, S, HALF):
-            product(1, (1,), lo, lo + HALF)
-
-        for lo in range(0, S, HALF):
-            for a in range(2):
-                weigh(a, lo, lo + HALF)
-        for a in range(2):
+        for i in range(S // PIECE):
+            product(0, (0, 1), i * PIECE, (i + 1) * PIECE, piece_out[i])
+        for a in (1, 0):
             for lo in range(0, S, HALF):
-                mix_and_store(a, lo, lo + HALF)
+                product(1, (a,), lo, lo + HALF, sigmoids_g[:, a : a + 1, lo : lo + HALF].rearrange("p a (r e) -> p a r e", e=SHARE))
+
+        for lo in range(0, S, HALF):
+            for a in (1, 0):
+                weigh(a, lo)
+        for a in (1, 0):
+            for lo in range(0, S, HALF):
+                mix_and_store(a, lo)

@@ -28,6 +28,8 @@ HALF = S // 2
 RUN = 4
 
 RAW = PACK * P
+POOL_SHARE = 48
+QUARTER = P // 4
 SHARE = P // 2
 
 
@@ -50,37 +52,20 @@ def tile_picked_zmos_sig_p_kernel(tc, x_words, x_scales, hT, gT, mix, offs, out)
         rounded_h = [sb.tile([P, P, PACK], BF16, name="rounded_h%d" % a, align_bytes=64) for a in range(2)]
         rounded_first = sb.tile([P, P, PACK], BF16, name="rounded_first", align_bytes=64)
 
-        shared = sb.tile([P, 4 * PACK, J], F32, name="shared", align_bytes=64)
+        groups = PIECE // QUARTER
+        shared = sb.tile([P, groups * 2 * PACK + 1, J], F32, name="shared", align_bytes=64)
         flat = shared[:].rearrange("p r c -> p (r c)")
-        raw_g = shared[:, PACK : 2 * PACK, :]
-        g_at = PACK * J
-        last_at = 2 * PACK * J - SHARE
+        g_row = (groups * 2 - 1) * PACK
+        raw_g = shared[:, g_row : g_row + PACK, :]
+        g_at = g_row * J
+        last_at = g_at + PACK * J - SHARE
         rounded_last = flat[:, last_at : last_at + RAW // 2].bitcast(BF16).rearrange("p (c j) -> p c j", j=PACK)
-        by_tile = shared[:, : 2 * PACK, P:].rearrange("p (a r) (u e) -> p a r u e", a=2, u=2)
-        late_at = (2 * PACK + 1) * J
-        piece_out = [
-            by_tile[:, :, 0:2, 0, :],
-            by_tile[:, :, 0:2, 1, :],
-            by_tile[:, :, 2, :, :],
-            flat[:, late_at : late_at + 2 * PIECE].rearrange("p (a u e) -> p a u e", a=2, u=2),
-        ]
-
-        def two_runs(first, second):
-            step = second - first
-            return flat[:, first : first + 2 * step].rearrange("p (r s) -> p r s", r=2)[:, :, :PIECE]
-
-        sigmoids_h = {}
-        for a in range(2):
-            sigmoids_h[a, 0] = by_tile[:, a, 0:2].rearrange("p r u e -> p u r e")
-            sigmoids_h[a, HALF] = two_runs((a * PACK + 2) * J + P, late_at + a * PIECE).rearrange("p r (u e) -> p r u e", u=2)
+        by_piece = shared[:, : groups * 2 * PACK, P : P + QUARTER].rearrange("p (k a i) e -> p a i k e", a=2, i=PACK)
+        piece_out = [by_piece[:, :, i] for i in range(S // PIECE)]
+        sigmoids_h = {(a, lo): by_piece[:, a, lo // PIECE : lo // PIECE + 2] for a in range(2) for lo in (0, HALF)}
         sigmoids_g = sb.tile([P, 2, S], F32, name="sigmoids_g", align_bytes=64)
-        weighted_late = sb.tile([P, 2, 2, PIECE], F32, name="weighted_late", align_bytes=64)
-        weighted = {
-            (1, 0): raw_g[:, 0:2, :P],
-            (0, 0): raw_g[:, 2:4, :P],
-            (1, HALF): weighted_late[:, 1],
-            (0, HALF): weighted_late[:, 0],
-        }
+        slots = shared[:, : groups * 2 * PACK, :SHARE].rearrange("p (r u a i) e -> p a i r u e", r=2, a=2, i=PACK)
+        weighted = {(1, 0): slots[:, 1, 0], (0, 0): slots[:, 1, 1], (1, HALF): slots[:, 1, 2], (0, HALF): slots[:, 1, 3]}
         stationary = {}
         for head in range(2):
             for a in range(2):
@@ -125,12 +110,12 @@ def tile_picked_zmos_sig_p_kernel(tc, x_words, x_scales, hT, gT, mix, offs, out)
                     start=True,
                     stop=True,
                 )
-            nc.scalar.activation(sigmoids, acc[:].rearrange("p a (r e) -> p a r e", e=SHARE), SIGMOID)
+            nc.scalar.activation(sigmoids, acc[:].rearrange("p a (r e) -> p a r e", e=QUARTER), SIGMOID)
 
         def weigh(a, lo):
             nc.vector.tensor_scalar(
-                weighted[a, lo].rearrange("p r (u e) -> p r u e", e=SHARE),
-                sigmoids_h[a, lo],
+                weighted[a, lo].rearrange("p r u (v e) -> p r u v e", v=2),
+                sigmoids_h[a, lo].rearrange("p r (u v) e -> p r u v e", v=2),
                 weights[:, a, 0:1],
                 None,
                 MULT,
@@ -139,8 +124,8 @@ def tile_picked_zmos_sig_p_kernel(tc, x_words, x_scales, hT, gT, mix, offs, out)
         def mix_and_store(a, lo):
             result = sb.tile([P, HALF], F32, name="result_%d_%d" % (a, lo))
             nc.vector.scalar_tensor_tensor(
-                result[:].rearrange("p (r s) -> p r s", r=2),
-                sigmoids_g[:, a, lo : lo + HALF].rearrange("p (r s) -> p r s", r=2),
+                result[:].rearrange("p (r u e) -> p r u e", r=2, u=2),
+                sigmoids_g[:, a, lo : lo + HALF].rearrange("p (r u e) -> p r u e", r=2, u=2),
                 weights[:, a, 1:2],
                 weighted[a, lo],
                 MULT,
@@ -174,19 +159,22 @@ def tile_picked_zmos_sig_p_kernel(tc, x_words, x_scales, hT, gT, mix, offs, out)
             columns = offsets[:, lo // LIST_GROUP : (lo + PIECE) // LIST_GROUP]
             nc.vector.tensor_copy(picked_words[:, lo : lo + PIECE], table_words[:].bitcast(U32).indirect(columns))
 
-        for lo in (0, SHARE):
-            round_tile(nc.scalar.copy, rounded_first[:, lo : lo + SHARE, :], raw_g[:, :, P + lo : P + lo + SHARE])
+        split = P - POOL_SHARE
+        for lo, hi in ((0, QUARTER), (QUARTER, split)):
+            round_tile(nc.scalar.copy, rounded_first[:, lo:hi, :], raw_g[:, :, P + lo : P + hi])
+        nc.gpsimd.tensor_scalar(
+            rounded_first[:, split:, :], raw_g[:, :, P + split :].rearrange("p j c -> p c j"), 1.0, 0.0, MULT, ADD
+        )
         round_tile(nc.vector.tensor_copy, rounded_last[:, SHARE:, :], raw_g[:, :, SHARE:P])
         quantize(1, 1, rounded_first[:], 0, P)
         round_tile(nc.vector.tensor_copy, rounded_last[:, :SHARE, :], raw_g[:, :, :SHARE])
-        quantize(1, 0, rounded_last[:, SHARE:, :], SHARE, P)
-        quantize(1, 0, rounded_last[:, :SHARE, :], 0, SHARE)
+        quantize(1, 0, rounded_last, 0, P)
 
         for i in range(S // PIECE):
             product(0, (0, 1), i * PIECE, (i + 1) * PIECE, piece_out[i])
         for a in (1, 0):
             for lo in range(0, S, HALF):
-                product(1, (a,), lo, lo + HALF, sigmoids_g[:, a : a + 1, lo : lo + HALF].rearrange("p a (r e) -> p a r e", e=SHARE))
+                product(1, (a,), lo, lo + HALF, sigmoids_g[:, a : a + 1, lo : lo + HALF].rearrange("p a (r e) -> p a r e", e=QUARTER))
 
         for lo in range(0, S, HALF):
             for a in (1, 0):

@@ -18,6 +18,7 @@ SIGMOID = mybir.ActivationFunctionType.Sigmoid
 
 P = 128
 PACK = 4
+PAIR = 2
 BLOCK = 32
 QUADRANT = 32
 ROWS = 4
@@ -26,11 +27,9 @@ BANKS = 8
 PIECE = 128
 HALF = S // 2
 RUN = 4
-
-RAW = PACK * P
-POOL_SHARE = 48
-QUARTER = P // 4
-SHARE = P // 2
+SLOT = 16
+FIRST = 2 * SLOT
+SHARE = 64
 
 
 def tile_picked_zmos_sig_p_kernel(tc, x_words, x_scales, hT, gT, mix, offs, out):
@@ -50,22 +49,18 @@ def tile_picked_zmos_sig_p_kernel(tc, x_words, x_scales, hT, gT, mix, offs, out)
 
         raw_h = sb.tile([P, PACK, J], F32, name="raw_h", align_bytes=64)
         rounded_h = [sb.tile([P, P, PACK], BF16, name="rounded_h%d" % a, align_bytes=64) for a in range(2)]
-        rounded_first = sb.tile([P, P, PACK], BF16, name="rounded_first", align_bytes=64)
+        rounded_g1 = sb.tile([P, P, PACK], BF16, name="rounded_g1", align_bytes=64)
 
-        groups = PIECE // QUARTER
-        shared = sb.tile([P, groups * 2 * PACK + 1, J], F32, name="shared", align_bytes=64)
+        rows = 2 * S // FIRST
+        shared = sb.tile([P, rows + 1, J], F32, name="shared", align_bytes=64)
         flat = shared[:].rearrange("p r c -> p (r c)")
-        g_row = (groups * 2 - 1) * PACK
-        raw_g = shared[:, g_row : g_row + PACK, :]
-        g_at = g_row * J
-        last_at = g_at + PACK * J - SHARE
-        rounded_last = flat[:, last_at : last_at + RAW // 2].bitcast(BF16).rearrange("p (c j) -> p c j", j=PACK)
-        by_piece = shared[:, : groups * 2 * PACK, P : P + QUARTER].rearrange("p (k a i) e -> p a i k e", a=2, i=PACK)
-        piece_out = [by_piece[:, :, i] for i in range(S // PIECE)]
-        sigmoids_h = {(a, lo): by_piece[:, a, lo // PIECE : lo // PIECE + 2] for a in range(2) for lo in (0, HALF)}
+        raw_g = shared[:, rows - PACK : rows, :]
+        g_at = (rows - PACK) * J
+        g0_at = rows * J - P + FIRST
+        rounded_g0 = flat[:, g0_at : g0_at + P * PACK // 2].bitcast(BF16).rearrange("p (c j) -> p c j", j=PACK)
+        slots = shared[:, :rows, P : P + FIRST].rearrange("p (a k h) (u e) -> p h u a k e", a=2, h=2, u=2)
         sigmoids_g = sb.tile([P, 2, S], F32, name="sigmoids_g", align_bytes=64)
-        slots = shared[:, : groups * 2 * PACK, :SHARE].rearrange("p (r u a i) e -> p a i r u e", r=2, a=2, i=PACK)
-        weighted = {(1, 0): slots[:, 1, 0], (0, 0): slots[:, 1, 1], (1, HALF): slots[:, 1, 2], (0, HALF): slots[:, 1, 3]}
+        weighted = shared[:, rows - 2 * PACK : rows, :P].rearrange("p (r a) (h e) -> p a h r e", a=2, h=2)
         stationary = {}
         for head in range(2):
             for a in range(2):
@@ -81,19 +76,15 @@ def tile_picked_zmos_sig_p_kernel(tc, x_words, x_scales, hT, gT, mix, offs, out)
                 in_=x_scales[0, r : K // BLOCK : ROWS, :].bitcast(I32),
             )
 
-        def round_tile(copy, rounded, raw):
+        def round_rows(copy, rounded, raw):
             copy(
                 rounded.rearrange("p (c i) j -> p c j i", i=RUN),
                 raw.rearrange("p j (c i) -> p c j i", i=RUN),
             )
 
-        def quantize(head, a, rounded, lo, hi):
+        def quantize(head, a, rounded):
             words, scales = stationary[head, a]
-            nc.vector.quantize_mx(
-                out=words[:, lo:hi].bitcast(FP8X4),
-                scales=scales[:, lo:hi],
-                in_=rounded.rearrange("p c j -> p (c j)"),
-            )
+            nc.vector.quantize_mx(out=words.bitcast(FP8X4), scales=scales, in_=rounded.rearrange("p c j -> p (c j)"))
 
         def product(head, tiles, lo, hi, sigmoids):
             n = len(products)
@@ -110,12 +101,12 @@ def tile_picked_zmos_sig_p_kernel(tc, x_words, x_scales, hT, gT, mix, offs, out)
                     start=True,
                     stop=True,
                 )
-            nc.scalar.activation(sigmoids, acc[:].rearrange("p a (r e) -> p a r e", e=QUARTER), SIGMOID)
+            nc.scalar.activation(sigmoids, acc[:].rearrange("p a (k e) -> p a k e", e=SLOT), SIGMOID)
 
         def weigh(a, lo):
             nc.vector.tensor_scalar(
-                weighted[a, lo].rearrange("p r u (v e) -> p r u v e", v=2),
-                sigmoids_h[a, lo].rearrange("p r (u v) e -> p r u v e", v=2),
+                weighted[:, a, lo // HALF].rearrange("p (u v) (k e) -> p u v k e", u=2, e=SLOT),
+                slots[:, lo // HALF, :, a].rearrange("p u (v k) e -> p u v k e", v=2),
                 weights[:, a, 0:1],
                 None,
                 MULT,
@@ -124,10 +115,10 @@ def tile_picked_zmos_sig_p_kernel(tc, x_words, x_scales, hT, gT, mix, offs, out)
         def mix_and_store(a, lo):
             result = sb.tile([P, HALF], F32, name="result_%d_%d" % (a, lo))
             nc.vector.scalar_tensor_tensor(
-                result[:].rearrange("p (r u e) -> p r u e", r=2, u=2),
-                sigmoids_g[:, a, lo : lo + HALF].rearrange("p (r u e) -> p r u e", r=2, u=2),
+                result[:].rearrange("p (r e) -> p r e", r=PACK),
+                sigmoids_g[:, a, lo : lo + HALF].rearrange("p (r e) -> p r e", r=PACK),
                 weights[:, a, 1:2],
-                weighted[a, lo],
+                weighted[:, a, lo // HALF],
                 MULT,
                 ADD,
             )
@@ -139,42 +130,45 @@ def tile_picked_zmos_sig_p_kernel(tc, x_words, x_scales, hT, gT, mix, offs, out)
         nc.gpsimd.memset(table_scales[:].bitcast(I32), 0)
 
         h_rows = hT.rearrange("(p j) c -> p j c", j=PACK)
-        nc.sync.dma_start(out=raw_h[:, : PACK // 2, :], in_=h_rows[:, : PACK // 2, :])
+        nc.sync.dma_start(out=raw_h[:, :PAIR, :], in_=h_rows[:, :PAIR, :])
         nc.sync.dma_start(offsets[:], offs)
         for r in range(ROWS // 2):
             load_scales(nc.sync, r)
             load_scales(nc.scalar, ROWS // 2 + r)
-        nc.sync.dma_start(out=raw_h[:, PACK // 2 :, :], in_=h_rows[:, PACK // 2 :, :])
+        nc.sync.dma_start(out=raw_h[:, PAIR:, :], in_=h_rows[:, PAIR:, :])
         nc.sync.dma_start(out=table_words[:], in_=x_words[0].rearrange("p n t -> p (n t)").bitcast(I32))
-        g_rows = gT.rearrange("(p j) c -> p (j c)", j=PACK)
-        nc.sync.dma_start(out=flat[:, g_at + P : g_at + PACK * J], in_=g_rows[:, P:])
-        nc.sync.dma_start(out=flat[:, g_at : g_at + P], in_=g_rows[:, :P])
+        g_runs = gT.rearrange("(p j) c -> p (j c)", j=PACK)
+        for j in range(0, PACK, PAIR):
+            lo, hi = j * J + P, (j + PAIR) * J
+            nc.sync.dma_start(out=flat[:, g_at + lo : g_at + hi], in_=g_runs[:, lo:hi])
+        nc.sync.dma_start(out=raw_g[:, 0:PACK:PAIR, :P], in_=gT.rearrange("(p j) c -> p j c", j=PACK)[:, 0:PACK:PAIR, :P])
         nc.sync.dma_start(out=weights[:], in_=mix.rearrange("(a p) c -> p a c", p=P))
 
+        for a in range(2):
+            round_rows(nc.scalar.copy, rounded_h[a][:, :, :PAIR], raw_h[:, :PAIR, a * P : (a + 1) * P])
         nc.vector.tensor_copy(picked_scales[:], table_scales[:].indirect(offsets[:]))
         for a in range(2):
-            round_tile(nc.scalar.copy, rounded_h[a][:], raw_h[:, :, a * P : (a + 1) * P])
-            quantize(0, a, rounded_h[a][:], 0, P)
+            round_rows(nc.scalar.copy, rounded_h[a][:, :, PAIR:], raw_h[:, PAIR:, a * P : (a + 1) * P])
+            quantize(0, a, rounded_h[a][:])
         for lo in range(0, S, PIECE):
             columns = offsets[:, lo // LIST_GROUP : (lo + PIECE) // LIST_GROUP]
             nc.vector.tensor_copy(picked_words[:, lo : lo + PIECE], table_words[:].bitcast(U32).indirect(columns))
 
-        split = P - POOL_SHARE
-        for lo, hi in ((0, QUARTER), (QUARTER, split)):
-            round_tile(nc.scalar.copy, rounded_first[:, lo:hi, :], raw_g[:, :, P + lo : P + hi])
+        round_rows(nc.scalar.copy, rounded_g1[:, :, :PAIR], raw_g[:, :PAIR, P:])
+        for lo, hi in ((0, FIRST), (FIRST, SHARE)):
+            round_rows(nc.scalar.copy, rounded_g1[:, lo:hi, PAIR:], raw_g[:, PAIR:, P + lo : P + hi])
         nc.gpsimd.tensor_scalar(
-            rounded_first[:, split:, :], raw_g[:, :, P + split :].rearrange("p j c -> p c j"), 1.0, 0.0, MULT, ADD
+            rounded_g1[:, SHARE:, PAIR:], raw_g[:, PAIR:, P + SHARE :].rearrange("p j c -> p c j"), 1.0, 0.0, MULT, ADD
         )
-        round_tile(nc.vector.tensor_copy, rounded_last[:, SHARE:, :], raw_g[:, :, SHARE:P])
-        quantize(1, 1, rounded_first[:], 0, P)
-        round_tile(nc.vector.tensor_copy, rounded_last[:, :SHARE, :], raw_g[:, :, :SHARE])
-        quantize(1, 0, rounded_last, 0, P)
+        quantize(1, 1, rounded_g1[:])
+        round_rows(nc.vector.tensor_copy, rounded_g0, raw_g[:, :, :P])
+        quantize(1, 0, rounded_g0)
 
         for i in range(S // PIECE):
-            product(0, (0, 1), i * PIECE, (i + 1) * PIECE, piece_out[i])
+            product(0, (0, 1), i * PIECE, (i + 1) * PIECE, slots[:, i // 2, i % 2])
         for a in (1, 0):
             for lo in range(0, S, HALF):
-                product(1, (a,), lo, lo + HALF, sigmoids_g[:, a : a + 1, lo : lo + HALF].rearrange("p a (r e) -> p a r e", e=QUARTER))
+                product(1, (a,), lo, lo + HALF, sigmoids_g[:, a : a + 1, lo : lo + HALF].rearrange("p a (k e) -> p a k e", e=SLOT))
 
         for lo in range(0, S, HALF):
             for a in (1, 0):

@@ -29,7 +29,7 @@ HALF = S // 2
 RUN = 4
 SLOT = 16
 FIRST = 2 * SLOT
-SHARE = 64
+SHARE = 96
 
 
 def tile_picked_zmos_sig_p_kernel(tc, x_words, x_scales, hT, gT, mix, offs, out):

@@ -27,9 +27,9 @@ BANKS = 8
 PIECE = 128
 HALF = S // 2
 RUN = 4
-SLOT = 16
-FIRST = 2 * SLOT
-SHARE = 96
+SLOT = 8
+FIRST = 4 * SLOT
+SHARE = 80
 
 
 def tile_picked_zmos_sig_p_kernel(tc, x_words, x_scales, hT, gT, mix, offs, out):
@@ -58,7 +58,7 @@ def tile_picked_zmos_sig_p_kernel(tc, x_words, x_scales, hT, gT, mix, offs, out)
         g_at = (rows - PACK) * J
         g0_at = rows * J - P + FIRST
         rounded_g0 = flat[:, g0_at : g0_at + P * PACK // 2].bitcast(BF16).rearrange("p (c j) -> p c j", j=PACK)
-        slots = shared[:, :rows, P : P + FIRST].rearrange("p (a k h) (u e) -> p h u a k e", a=2, h=2, u=2)
+        slots = shared[:, :rows, P : P + FIRST].rearrange("p (k h) (u a e) -> p h u a k e", a=2, h=2, u=2)
         sigmoids_g = sb.tile([P, 2, S], F32, name="sigmoids_g", align_bytes=64)
         weighted = shared[:, rows - 2 * PACK : rows, :P].rearrange("p (r a) (h e) -> p a h r e", a=2, h=2)
         stationary = {}
@@ -112,16 +112,17 @@ def tile_picked_zmos_sig_p_kernel(tc, x_words, x_scales, hT, gT, mix, offs, out)
                 MULT,
             )
 
-        def mix_and_store(a, lo):
+        def mix_and_store(a, lo, step):
             result = sb.tile([P, HALF], F32, name="result_%d_%d" % (a, lo))
-            nc.vector.scalar_tensor_tensor(
-                result[:].rearrange("p (r e) -> p r e", r=PACK),
-                sigmoids_g[:, a, lo : lo + HALF].rearrange("p (r e) -> p r e", r=PACK),
-                weights[:, a, 1:2],
-                weighted[:, a, lo // HALF],
-                MULT,
-                ADD,
-            )
+            for at in range(0, HALF, step):
+                nc.vector.scalar_tensor_tensor(
+                    result[:, at : at + step].rearrange("p (r e) -> p r e", e=P // 2),
+                    sigmoids_g[:, a, lo + at : lo + at + step].rearrange("p (r e) -> p r e", e=P // 2),
+                    weights[:, a, 1:2],
+                    weighted[:, a, lo // HALF, at // (P // 2) : (at + step) // (P // 2)],
+                    MULT,
+                    ADD,
+                )
             nc.sync.dma_start(out=out[a * P : (a + 1) * P, lo : lo + HALF], in_=result[:])
 
         nc.vector.memset(warm_in[:], 0.0)
@@ -165,14 +166,15 @@ def tile_picked_zmos_sig_p_kernel(tc, x_words, x_scales, hT, gT, mix, offs, out)
         quantize(1, 0, rounded_g0)
 
         for i in range(S // PIECE):
-            product(0, (0, 1), i * PIECE, (i + 1) * PIECE, slots[:, i // 2, i % 2])
-        for a in (1, 0):
-            for lo in range(0, S, HALF):
-                product(1, (a,), lo, lo + HALF, sigmoids_g[:, a : a + 1, lo : lo + HALF].rearrange("p a (k e) -> p a k e", e=SLOT))
+            for a in (1, 0):
+                product(0, (a,), i * PIECE, (i + 1) * PIECE, slots[:, i // 2, i % 2, a : a + 1])
+        for a, step in ((1, PIECE), (0, PIECE)):
+            for lo in range(0, S, step):
+                product(1, (a,), lo, lo + step, sigmoids_g[:, a : a + 1, lo : lo + step].rearrange("p a (k e) -> p a k e", e=SLOT))
 
         for lo in range(0, S, HALF):
             for a in (1, 0):
                 weigh(a, lo)
-        for a in (1, 0):
+        for a, step in ((1, PIECE), (0, PIECE)):
             for lo in range(0, S, HALF):
-                mix_and_store(a, lo)
+                mix_and_store(a, lo, step)

@@ -29,7 +29,7 @@ HALF = S // 2
 RUN = 4
 SLOT = 8
 FIRST = 4 * SLOT
-SHARE = 80
+SHARE = 48
 
 
 def tile_picked_zmos_sig_p_kernel(tc, x_words, x_scales, hT, gT, mix, offs, out):

@@ -29,6 +29,7 @@ HALF = S // 2
 RUN = 4
 SLOT = 8
 FIRST = 4 * SLOT
+H_SHARE = 32
 SHARE = 48
 
 
@@ -44,10 +45,9 @@ def tile_picked_zmos_sig_p_kernel(tc, x_words, x_scales, hT, gT, mix, offs, out)
         weights = sb.tile([P, 2, 2], F32, name="weights", align_bytes=64)
         warm_in = sb.tile([P, 1], F32, name="warm_in")
         warm_out = sb.tile([P, 1], F32, name="warm_out")
-        picked_words = sb.tile([P, S], U32, name="picked_words", align_bytes=64)
         picked_scales = sb.tile([P, S], U8, name="picked_scales", align_bytes=64)
 
-        raw_h = sb.tile([P, PACK, J], F32, name="raw_h", align_bytes=64)
+        raw_h = sb.tile([P, PACK, J], F32, name="raw_h", tag="raw_h", align_bytes=64)
         rounded_h = [sb.tile([P, P, PACK], BF16, name="rounded_h%d" % a, align_bytes=64) for a in range(2)]
         rounded_g1 = sb.tile([P, P, PACK], BF16, name="rounded_g1", align_bytes=64)
 
@@ -145,12 +145,15 @@ def tile_picked_zmos_sig_p_kernel(tc, x_words, x_scales, hT, gT, mix, offs, out)
         nc.sync.dma_start(out=raw_g[:, 0:PACK:PAIR, :P], in_=gT.rearrange("(p j) c -> p j c", j=PACK)[:, 0:PACK:PAIR, :P])
         nc.sync.dma_start(out=weights[:], in_=mix.rearrange("(a p) c -> p a c", p=P))
 
-        for a in range(2):
-            round_rows(nc.scalar.copy, rounded_h[a][:, :, :PAIR], raw_h[:, :PAIR, a * P : (a + 1) * P])
         nc.vector.tensor_copy(picked_scales[:], table_scales[:].indirect(offsets[:]))
-        for a in range(2):
-            round_rows(nc.scalar.copy, rounded_h[a][:, :, PAIR:], raw_h[:, PAIR:, a * P : (a + 1) * P])
+        round_rows(nc.scalar.copy, rounded_h[1][:], raw_h[:, :, P:])
+        round_rows(nc.scalar.copy, rounded_h[0][:, :H_SHARE, :], raw_h[:, :, :H_SHARE])
+        nc.gpsimd.tensor_scalar(
+            rounded_h[0][:, H_SHARE:, :], raw_h[:, :, H_SHARE:P].rearrange("p j c -> p c j"), 1.0, 0.0, MULT, ADD
+        )
+        for a in (1, 0):
             quantize(0, a, rounded_h[a][:])
+        picked_words = sb.tile([P, S], U32, name="picked_words", tag="raw_h", align_bytes=64)
         for lo in range(0, S, PIECE):
             columns = offsets[:, lo // LIST_GROUP : (lo + PIECE) // LIST_GROUP]
             nc.vector.tensor_copy(picked_words[:, lo : lo + PIECE], table_words[:].bitcast(U32).indirect(columns))

@@ -29,6 +29,7 @@ HALF = S // 2
 RUN = 4
 SLOT = 8
 FIRST = 4 * SLOT
+LAST = 4 * S // PIECE - 1
 H_SHARE = 32
 SHARE = 48
 
@@ -101,7 +102,12 @@ def tile_picked_zmos_sig_p_kernel(tc, x_words, x_scales, hT, gT, mix, offs, out)
                     start=True,
                     stop=True,
                 )
-            nc.scalar.activation(sigmoids, acc[:].rearrange("p a (k e) -> p a k e", e=SLOT), SIGMOID)
+            runs = (hi - lo) // SLOT
+            cuts = (0, runs // 2, runs) if n == LAST else (0, runs)
+            for first, end in zip(cuts, cuts[1:]):
+                nc.scalar.activation(
+                    sigmoids[:, :, first:end], acc[:].rearrange("p a (k e) -> p a k e", e=SLOT)[:, :, first:end], SIGMOID
+                )
 
         def weigh(a, lo):
             nc.vector.tensor_scalar(
@@ -114,12 +120,13 @@ def tile_picked_zmos_sig_p_kernel(tc, x_words, x_scales, hT, gT, mix, offs, out)
 
         def mix_and_store(a, lo, step):
             result = sb.tile([P, HALF], F32, name="result_%d_%d" % (a, lo))
-            for at in range(0, HALF, step):
+            cuts = (0, step, HALF - step // 2, HALF) if (a, lo) == (0, HALF) else (0, step, HALF)
+            for at, to in zip(cuts, cuts[1:]):
                 nc.vector.scalar_tensor_tensor(
-                    result[:, at : at + step].rearrange("p (r e) -> p r e", e=P // 2),
-                    sigmoids_g[:, a, lo + at : lo + at + step].rearrange("p (r e) -> p r e", e=P // 2),
+                    result[:, at:to].rearrange("p (r e) -> p r e", e=P // 2),
+                    sigmoids_g[:, a, lo + at : lo + to].rearrange("p (r e) -> p r e", e=P // 2),
                     weights[:, a, 1:2],
-                    weighted[:, a, lo // HALF, at // (P // 2) : (at + step) // (P // 2)],
+                    weighted[:, a, lo // HALF, at // (P // 2) : to // (P // 2)],
                     MULT,
                     ADD,
                 )

from contextlib import ExitStack

import concourse.mybir as mybir

K, T, S, J = 512, 1024, 512, 256
FLOPS = 2 * 2 * K * J * S

F32 = mybir.dt.float32
BF16 = mybir.dt.bfloat16
I32 = mybir.dt.int32
U32 = mybir.dt.uint32
U16 = mybir.dt.uint16
U8 = mybir.dt.uint8
FP8X4 = mybir.dt.float8_e4m3fn_x4
MULT = mybir.AluOpType.mult
ADD = mybir.AluOpType.add
SIGMOID = mybir.ActivationFunctionType.Sigmoid

P = 128
PACK = 4
PAIR = 2
BLOCK = 32
QUADRANT = 32
ROWS = 4
LIST_GROUP = 16
BANKS = 8
PIECE = 128
HALF = S // 2
RUN = 4
SLOT = 8
FIRST = 4 * SLOT
LAST = 4 * S // PIECE - 1
H_SHARE = 32
SHARE = 48


def tile_picked_zmos_sig_p_kernel(tc, x_words, x_scales, hT, gT, mix, offs, out):
    nc = tc.nc
    with ExitStack() as ctx:
        sb = ctx.enter_context(tc.tile_pool(name="sb", bufs=1))
        ps = ctx.enter_context(tc.psum_pool(name="ps", bufs=1))

        offsets = sb.tile([P, S // LIST_GROUP], U16, name="offsets")
        table_scales = sb.tile([P, T], U8, name="table_scales", align_bytes=64)
        table_words = sb.tile([P, T], I32, name="table_words", align_bytes=64)
        weights = sb.tile([P, 2, 2], F32, name="weights", align_bytes=64)
        warm_in = sb.tile([P, 1], F32, name="warm_in")
        warm_out = sb.tile([P, 1], F32, name="warm_out")
        picked_scales = sb.tile([P, S], U8, name="picked_scales", align_bytes=64)

        raw_h = sb.tile([P, PACK, J], F32, name="raw_h", tag="raw_h", align_bytes=64)
        rounded_h = [sb.tile([P, P, PACK], BF16, name="rounded_h%d" % a, align_bytes=64) for a in range(2)]
        rounded_g1 = sb.tile([P, P, PACK], BF16, name="rounded_g1", align_bytes=64)

        rows = 2 * S // FIRST
        shared = sb.tile([P, rows + 1, J], F32, name="shared", align_bytes=64)
        flat = shared[:].rearrange("p r c -> p (r c)")
        raw_g = shared[:, rows - PACK : rows, :]
        g_at = (rows - PACK) * J
        g0_at = rows * J - P + FIRST
        rounded_g0 = flat[:, g0_at : g0_at + P * PACK // 2].bitcast(BF16).rearrange("p (c j) -> p c j", j=PACK)
        slots = shared[:, :rows, P : P + FIRST].rearrange("p (k h) (u a e) -> p h u a k e", a=2, h=2, u=2)
        sigmoids_g = sb.tile([P, 2, S], F32, name="sigmoids_g", align_bytes=64)
        weighted = shared[:, rows - 2 * PACK : rows, :P].rearrange("p (r a) (h e) -> p a h r e", a=2, h=2)
        stationary = {}
        for head in range(2):
            for a in range(2):
                stationary[head, a] = (
                    sb.tile([P, P], U32, name="words_%d_%d" % (head, a), align_bytes=64)[:],
                    sb.tile([P, P], U8, name="scales_%d_%d" % (head, a), align_bytes=64)[:],
                )
        products = []

        def load_scales(queue, r):
            queue.dma_start(
                out=table_scales[r:P:QUADRANT, :].bitcast(I32),
                in_=x_scales[0, r : K // BLOCK : ROWS, :].bitcast(I32),
            )

        def round_rows(copy, rounded, raw):
            copy(
                rounded.rearrange("p (c i) j -> p c j i", i=RUN),
                raw.rearrange("p j (c i) -> p c j i", i=RUN),
            )

        def quantize(head, a, rounded):
            words, scales = stationary[head, a]
            nc.vector.quantize_mx(out=words.bitcast(FP8X4), scales=scales, in_=rounded.rearrange("p c j -> p (c j)"))

        def product(head, tiles, lo, hi, sigmoids):
            n = len(products)
            acc = ps.tile([P, len(tiles), hi - lo], F32, name="acc_%d" % n, tag="bank_%d" % (n % BANKS))
            products.append(acc)
            for i, a in enumerate(tiles):
                words, scales = stationary[head, a]
                nc.tensor.matmul_mx(
                    out=acc[:, i, :],
                    lhsT=words.bitcast(FP8X4),
                    lhsT_scale=scales,
                    rhs=picked_words[:, lo:hi].bitcast(FP8X4),
                    rhs_scale=picked_scales[:, lo:hi],
                    start=True,
                    stop=True,
                )
            runs = (hi - lo) // SLOT
            cuts = (0, runs // 2, runs) if n == LAST else (0, runs)
            for first, end in zip(cuts, cuts[1:]):
                nc.scalar.activation(
                    sigmoids[:, :, first:end], acc[:].rearrange("p a (k e) -> p a k e", e=SLOT)[:, :, first:end], SIGMOID
                )

        def weigh(a, lo):
            nc.vector.tensor_scalar(
                weighted[:, a, lo // HALF].rearrange("p (u v) (k e) -> p u v k e", u=2, e=SLOT),
                slots[:, lo // HALF, :, a].rearrange("p u (v k) e -> p u v k e", v=2),
                weights[:, a, 0:1],
                None,
                MULT,
            )

        def mix_and_store(a, lo, step):
            result = sb.tile([P, HALF], F32, name="result_%d_%d" % (a, lo))
            cuts = (0, step, HALF - step // 2, HALF) if (a, lo) == (0, HALF) else (0, step, HALF)
            for at, to in zip(cuts, cuts[1:]):
                nc.vector.scalar_tensor_tensor(
                    result[:, at:to].rearrange("p (r e) -> p r e", e=P // 2),
                    sigmoids_g[:, a, lo + at : lo + to].rearrange("p (r e) -> p r e", e=P // 2),
                    weights[:, a, 1:2],
                    weighted[:, a, lo // HALF, at // (P // 2) : to // (P // 2)],
                    MULT,
                    ADD,
                )
            nc.sync.dma_start(out=out[a * P : (a + 1) * P, lo : lo + HALF], in_=result[:])

        nc.vector.memset(warm_in[:], 0.0)
        nc.scalar.activation(warm_out[:], warm_in[:], SIGMOID)

        nc.gpsimd.memset(table_scales[:].bitcast(I32), 0)

        h_rows = hT.rearrange("(p j) c -> p j c", j=PACK)
        nc.sync.dma_start(out=raw_h[:, :PAIR, :], in_=h_rows[:, :PAIR, :])
        nc.sync.dma_start(offsets[:], offs)
        for r in range(ROWS // 2):
            load_scales(nc.sync, r)
            load_scales(nc.scalar, ROWS // 2 + r)
        nc.sync.dma_start(out=raw_h[:, PAIR:, :], in_=h_rows[:, PAIR:, :])
        nc.sync.dma_start(out=table_words[:], in_=x_words[0].rearrange("p n t -> p (n t)").bitcast(I32))
        g_runs = gT.rearrange("(p j) c -> p (j c)", j=PACK)
        for j in range(0, PACK, PAIR):
            lo, hi = j * J + P, (j + PAIR) * J
            nc.sync.dma_start(out=flat[:, g_at + lo : g_at + hi], in_=g_runs[:, lo:hi])
        nc.sync.dma_start(out=raw_g[:, 0:PACK:PAIR, :P], in_=gT.rearrange("(p j) c -> p j c", j=PACK)[:, 0:PACK:PAIR, :P])
        nc.sync.dma_start(out=weights[:], in_=mix.rearrange("(a p) c -> p a c", p=P))

        nc.vector.tensor_copy(picked_scales[:], table_scales[:].indirect(offsets[:]))
        round_rows(nc.scalar.copy, rounded_h[1][:], raw_h[:, :, P:])
        round_rows(nc.scalar.copy, rounded_h[0][:, :H_SHARE, :], raw_h[:, :, :H_SHARE])
        nc.gpsimd.tensor_scalar(
            rounded_h[0][:, H_SHARE:, :], raw_h[:, :, H_SHARE:P].rearrange("p j c -> p c j"), 1.0, 0.0, MULT, ADD
        )
        for a in (1, 0):
            quantize(0, a, rounded_h[a][:])
        picked_words = sb.tile([P, S], U32, name="picked_words", tag="raw_h", align_bytes=64)
        for lo in range(0, S, PIECE):
            columns = offsets[:, lo // LIST_GROUP : (lo + PIECE) // LIST_GROUP]
            nc.vector.tensor_copy(picked_words[:, lo : lo + PIECE], table_words[:].bitcast(U32).indirect(columns))

        round_rows(nc.scalar.copy, rounded_g1[:, :, :PAIR], raw_g[:, :PAIR, P:])
        for lo, hi in ((0, FIRST), (FIRST, SHARE)):
            round_rows(nc.scalar.copy, rounded_g1[:, lo:hi, PAIR:], raw_g[:, PAIR:, P + lo : P + hi])
        nc.gpsimd.tensor_scalar(
            rounded_g1[:, SHARE:, PAIR:], raw_g[:, PAIR:, P + SHARE :].rearrange("p j c -> p c j"), 1.0, 0.0, MULT, ADD
        )
        quantize(1, 1, rounded_g1[:])
        round_rows(nc.vector.tensor_copy, rounded_g0, raw_g[:, :, :P])
        quantize(1, 0, rounded_g0)

        for i in range(S // PIECE):
            for a in (1, 0):
                product(0, (a,), i * PIECE, (i + 1) * PIECE, slots[:, i // 2, i % 2, a : a + 1])
        for a, step in ((1, PIECE), (0, PIECE)):
            for lo in range(0, S, step):
                product(1, (a,), lo, lo + step, sigmoids_g[:, a : a + 1, lo : lo + step].rearrange("p a (k e) -> p a k e", e=SLOT))

        for lo in range(0, S, HALF):
            for a in (1, 0):
                weigh(a, lo)
        for a, step in ((1, PIECE), (0, PIECE)):
            for lo in range(0, S, HALF):
                mix_and_store(a, lo, step)
